import numpy as np, ml_dtypes
CORES = [1,5,17,21,33,37,49,53]
N = 8
BF = ml_dtypes.bfloat16
W, V, L, S, T, E = 4096, 1024, 128, 32, 5, 2
def parts(rng):
    x = (64 * rng.random((N, 8, 16, W)) * (0.5 + 0.5 * rng.random((N, 8, 1, W)))).astype(np.int64)
    im = (64 * rng.random((N, 8, 16, V)) * (0.25 + 0.75 * rng.random((N, 8, 1, V)))).astype(np.int64)
    z = (64 * rng.random((N, 8, 16, 2, L)) * (0.5 + 0.5 * rng.random((N, 8, 1, 2, L)))).astype(np.int64)
    b = rng.integers(0, W, (N, 8, 16, V)); q = np.minimum((8 * rng.random((N, 8, 16, V)) ** 0.6).astype(np.int64), 7)
    return x, im, b, q, z, rng.integers(1, 4096, (N, 8, 16))
def pack(x, im, b, q, z, w):
    return {"geno": x.reshape(N, 128, W).astype(np.float32).astype(BF), "immun": im.reshape(N, 128, V).astype(np.float32).astype(BF),
            "bank": (b + W * q).reshape(N, 128, V).astype(np.int32), "bites": z.reshape(N, 128, 2 * L).astype(np.float32).astype(BF), "wt": w.reshape(N, 128, 1).astype(np.int32)}
def first(z, w):
    u = np.sum(w[:, :, :, None] * z[:, :, :, 0], axis=2) & 4095
    return ((u * u >> 5) + 37 * u) & (V - 1)
def setup_inputs(rng):
    return pack(*parts(rng))
def setup_inputs_corners(rng):
    x, im, b, q, z, w = parts(rng); w[:, :, 0] = 4095; w[:, :, 1] = 2048
    kind = rng.integers(0, 4, (N, 8, 1, V)); im = np.where(kind == 0, 0, np.where(kind == 1, 63, im))
    mode = rng.integers(0, 7, (N, 8, 1, V)); pos = np.argsort(rng.random((N, 8, 16, V)), axis=2); near = E - 1 + rng.integers(0, 3, q.shape)
    q = np.where(mode == 5, q[:, :, :1], q); q = np.where(mode == 4, near, q); q = np.where(mode == 3, 7 * (pos < 2), q)
    q = np.where(mode == 2, 7 * (pos < 1), q); q = np.where(mode == 1, 0, q); q = np.where(mode == 0, 7, q)
    edge = rng.integers(0, 4, (N, 8, 1, V)); b = np.where(edge == 0, (W - 1) * rng.integers(0, 2, b.shape), b); b = np.where(edge == 1, b[:, :, :1], b)
    z[:, :, :, 0, 4:L - 1] = np.maximum(z[:, :, :, 0, 4:L - 1], 1)
    z[:, :, :, :, 0] = 0; z[:, :, :, :, 1] = 63; z[:, :, :, :, 2] = 0; z[:, :, 1, :, 2] = 1; z[:, :, :, :, L - 1] = 0; z[:, :, 0, :, L - 1] = 1
    v = first(z, w); n = L // 2; m = L // 8
    for a in range(N):
        for g in range(8):
            lanes = (4 + rng.permutation(L - 5))[:n]; zz = z[a, g, :, 0][:, lanes]
            po = np.argsort(rng.random((16, n)), axis=0); cnt = 8 + np.arange(n) % 3
            im[a, g][:, v[a, g, lanes]] = zz - (po < cnt)
            own = lanes[:m]; k = rng.integers(0, 16, m); h = v[a, g, own]
            b[a, g, k, h] = S * own; q[a, g, k, h] = 7
            x[a, g][:, S * own] = np.where(zz[:, :m] < 32, 63, 0)
    return pack(x, im, b, q, z, w)
def setup_inputs_crowd(rng):
    x, im, b, q, z, w = parts(rng); w = np.repeat(rng.integers(1, 4096, (N, 8, 1)), 16, axis=2)
    for a in range(N):
        for g in range(8):
            for c in range(2):
                n = int(rng.choice(np.array([1, 2, 5, 17, 30])))
                if g == a % 8 and c == 0: n = 1
                if g == (a + 3) % 8 and c == 0: continue
                base = z[a, g, :, c, :n].copy()[:, rng.integers(0, n, L)]
                z[a, g, :, c] = np.take_along_axis(base, np.argsort(rng.random((16, L)), axis=0), 0)
        g = (a + 3) % 8; w[a, g] = rng.integers(1, 4096, 16); w[a, g, 0] = 1; w[a, g, 15] = 64
        u = rng.permutation(4096); u = u[np.unique(((u * u >> 5) + 37 * u) & (V - 1), return_index=True)[1]]
        need = (rng.permutation(u)[:L] - np.sum(w[a, g, 1:15, None] * z[a, g, 1:15, 0], axis=0)) & 4095
        z[a, g, 0, 0] = need & 63; z[a, g, 15, 0] = need >> 6
    return pack(x, im, b, q, z, w)
def setup_inputs_ends(rng):
    def rec(n):
        k = rng.integers(0, 3, (N, 8, 1, n)); return 63 * np.where(k == 2, rng.integers(0, 2, (N, 8, 16, n)), k)
    x = rec(W); im = rec(V); z = rec(2 * L).reshape(N, 8, 16, 2, L); w = np.where(rng.integers(0, 2, (N, 8, 16)) == 1, 4095, 1); w[N - 1, 7] = 4095
    x[:, 1::2, :, W - 1] = 0; x[:, ::2, :, W - 1] = 63 * rng.integers(0, 2, (N, 4, 16))
    nz = rng.integers(0, 8, (8, 1, L)) * rng.integers(0, 2, (8, 1, L)); nz[:, :, 0] = 0; nz[:, :, L - 1] = 0
    nz[0, 0, ::2] = 0; nz[0, 0, 1] = 1; nz[0, 0, L - 1] = 0
    z[N - 1, :, :, 0] = 63 * (np.argsort(rng.random((8, 16, L)), axis=1) >= nz)
    z[1, :, :, 0] = 63 * (np.argsort(rng.random((8, 16, L)), axis=1) >= rng.integers(0, 8, (8, 1, L)))
    v = first(z, w); r = np.arange(16)[None, None, :, None]; mode = rng.integers(0, 5, (N, 8, 1, V))
    fl = (mode == 0) | ((mode == 1) & (r >= 14)) | ((mode == 2) & ((r == 0) | (r == 15))) | ((mode == 4) & (rng.random((N, 8, 16, V)) < 0.5))
    anyb = (rng.random((N, 8, 1, V)) < 0.5) & fl
    for g in range(8):
        for a in (1, N - 1):
            h = v[a, g]; fl[a, g, 14:][:, h] = True; anyb[a, g][:, h] = False; im[a, g][:, h] = 0
        im[0, g][:, v[0, g]] = 63
    im[N - 1, 0][:, v[N - 1, 0, 1]] = 63
    woke = 16 * L - 2 * int(np.sum(v[N - 1, 0] == v[N - 1, 0, 1])); assert woke > 15 * L and woke & (V - 1) != 0
    b = np.where(fl, np.where(anyb, rng.integers(0, W, fl.shape), W - 1), 0); q = 7 * fl
    for g, ks in ((1, (2, 5, 9)), (3, (0, 1, 15)), (5, (13, 14, 15))):
        h = v[N - 1, g, 0]; x[N - 1, g, :, W - 2] = 0; x[N - 1, g, rng.integers(0, 16), W - 2] = 1
        b[N - 1, g, :, h] = 0; q[N - 1, g, :, h] = 0
        for k, c in zip(ks, (W - 2, W - 2, W - 1)):
            b[N - 1, g, k, h] = c; q[N - 1, g, k, h] = 7
    return pack(x, im, b, q, z, w)
def setup_inputs_spread(rng):
    x, im, b, q, z, w = parts(rng)
    def pw(*s): return rng.random(s) ** np.exp2(rng.integers(-2, 4, s[:2] + (1,) + s[3:]))
    x = np.minimum((64 * pw(N, 8, 16, W)).astype(np.int64), 63); im = np.minimum((64 * pw(N, 8, 16, V)).astype(np.int64), 63)
    z = np.minimum((64 * pw(N, 8, 16, 2, L)).astype(np.int64), 63); b = np.minimum((W * pw(N, 8, 16, V)).astype(np.int64), W - 1)
    q = np.minimum((8 * rng.random((N, 8, 16, V)) ** np.exp2(rng.integers(-2, 2, (N, 8, 1, V)))).astype(np.int64), 7)
    w = np.minimum(np.exp2(12 * rng.random((N, 8, 16))).astype(np.int64), 4095)
    return pack(x, im, b, q, z, np.maximum(w, 1))
def setup_inputs_ties(rng):
    lv = rng.integers(0, 3, (N, 8, 1, W)); x = lv + rng.integers(0, 3, (N, 8, 16, W)); im = rng.integers(0, 3, (N, 8, 16, V))
    z = rng.integers(0, 3, (N, 8, 1, 2, L)) + rng.integers(0, 3, (N, 8, 16, 2, L)); w = rng.integers(1, 4096, (N, 8, 16)); b = rng.integers(0, W, (N, 8, 16, V))
    q = np.where(rng.random((N, 8, 16, V)) < 0.5, rng.integers(0, 8, (N, 8, 1, V)), rng.integers(4, 8, (N, 8, 1, V)))
    x[:, ::2, :, W // 2:] = x[:, ::2, :, :W // 2]; b[:, :, 8:, ::2] = b[:, :, :8, ::2]
    z[:, :, :, 0, ::4] = np.take_along_axis(x, rng.integers(0, W, (N, 8, 1, L // 4)), 3)
    x[:, 1::2] += 59; im[:, 1::2] += 59; z[:, 1::2] += 59
    r = np.arange(16)[:, None]; x[:, 2] = (r + np.arange(W)) % 3; z[:, 2, :, 0] = (r + np.arange(L)) % 3; im[:, 2] = 0
    same = ((4, 0, [15]), (6, L // 2, [2, 15]), (7, L - 1, [15])); cz = rng.integers(0, W, (N, 8))
    for a in range(N):
        for g, j, ks in same:
            e = 59 * (g % 2) + rng.integers(1, 3, 16); z[a, g, :, 0, j] = e; x[a, g, :, cz[a, g]] = e
    v = first(z, w)
    for a in range(N):
        for j in range(3):
            h = v[a, 2, j]; q[a, 2, :, h] = 0; q[a, 2, 3, h] = 7; q[a, 2, 12, h] = 7
            b[a, 2, 3, h] = 3 * rng.integers(0, W // 3) + (j + 1) % 3; b[a, 2, 12, h] = 3 * rng.integers(0, W // 3) + (j + 2) % 3
        for g, j, ks in same:
            h = v[a, g, j]; im[a, g, :, h] = 0; q[a, g, :, h] = 0; b[a, g, 15, h] = cz[a, g]
            for k in ks: q[a, g, k, h] = 7
    return pack(x, im, b, q, z, w)
def check_inputs(d):
    bad = []
    for k, lo, hi in (("geno", 0, 63), ("immun", 0, 63), ("bank", 0, 8 * W - 1), ("bites", 0, 63), ("wt", 1, 4095)):
        a = np.asarray(d[k]).astype(np.float64)
        if not np.all((a >= lo) & (a <= hi)): bad.append("range of " + k)
        elif np.any(a != np.floor(a)): bad.append("whole numbers of " + k)
    return bad
def beats(a, c):
    return (np.sum(a > c, axis=2) >= 9).astype(np.int64)
def reference(geno, immun, bank, bites, wt):
    X = geno.astype(np.float32).astype(np.int64).reshape(N, 8, 16, W); im = immun.astype(np.float32).astype(np.int64).reshape(N, 8, 16, V)
    bk = bank.astype(np.int64).reshape(N, 8, 16, V); z = bites.astype(np.float32).astype(np.int64).reshape(N, 8, 16, 2, L); w = wt.astype(np.int64).reshape(N, 8, 16, 1)
    todo = [z[:, :, :, 0], np.roll(z[:, :, :, 1], 1, axis=0)]
    A = np.zeros(N, np.int64); row = np.arange(16)[None, None, :, None]; lane = np.arange(L)[None, None, None, :]
    for t in range(T):
        s = todo[t]
        u = np.sum(w * s, axis=2) & 4095; v = ((u * u >> 5) + 37 * u + A[:, None, None]) & (V - 1)
        e = np.take_along_axis(bk, v[:, :, None, :], 3); b = e & (W - 1); q = e // W
        iv = np.take_along_axis(im, v[:, :, None, :], 3)
        c = np.take_along_axis(X, b.reshape(N, 8, 1, 16 * L), 3).reshape(N, 8, 16, 16, L)
        D = np.sum(np.abs(c - s[:, :, :, None, :]), axis=2)
        sick = np.sum(s > iv, axis=2) >= 9
        key = np.where((q >= t + E) & sick[:, :, None, :], D * 16 + 15 - row, -1)
        k1 = np.argmax(key, axis=2); h1 = (np.max(key, axis=2) >= 0).astype(np.int64)
        key = np.where(row == k1[:, :, None, :], -1, key)
        k2 = np.argmax(key, axis=2); h2 = (np.max(key, axis=2) >= 0).astype(np.int64)
        a1 = np.take_along_axis(c, k1[:, :, None, None, :], 3)[:, :, :, 0]; a2 = np.take_along_axis(c, k2[:, :, None, None, :], 3)[:, :, :, 0]
        n0 = h1 * beats(a1, s) + h2 * beats(a2, s); n1 = beats(s, a1) + h2 * beats(a2, a1); n2 = beats(s, a2) + beats(a1, a2)
        o = np.argsort(np.stack([n0 * 4, np.where(h1 == 1, n1 * 4 + 1, 97), np.where(h2 == 1, n2 * 4 + 2, 98)]), axis=0)
        st = np.stack([s, a1, a2]); second = np.where(h1 == 1, o[1], 0)
        f = np.take_along_axis(st, o[0][None, :, :, None, :], 0)[0]; m = np.take_along_axis(st, second[None, :, :, None, :], 0)[0]
        todo.append(np.roll(np.where((u[:, :, None, :] >> (row & 7)) & 1 == 1, f, m), 2, axis=0))
        wake = ((row == k1[:, :, None, :]) & (h1[:, :, None, :] == 1)) | ((row == k2[:, :, None, :]) & (h2[:, :, None, :] == 1))
        q = np.where(wake, 0, q); slot = np.argmin(q * 16 + row, axis=2)
        e = np.where(row == slot[:, :, None, :], S * lane + t + W * (8 + t), b + W * q); iv = np.maximum(iv - 1, f)
        for a in range(N):
            for g in range(8):
                hv, fi = np.unique(v[a, g], return_index=True)
                bk[a, g][:, hv] = e[a, g][:, fi]; im[a, g][:, hv] = iv[a, g][:, fi]
        X[:, :, :, t::S] = s
        A = np.sum(h1 + h2, axis=(1, 2))
    return {"ybank": bk.reshape(N, 128, V).astype(np.float32), "yimm": im.reshape(N, 128, V).astype(np.float32).astype(BF), "ygeno": X.reshape(N, 128, W).astype(np.float32).astype(BF)}

@@ -1,0 +1,623 @@
+import numpy as np
+from concourse.mybir import AluOpType as OP, AxisListType, ActivationFunctionType as AF
+
+NST = 5
+XS = 257
+THR = 16384.0
+BIG = 2.0 ** 20
+ON_DVE = (0, 2, 4, 6)
+
+SCRATCH = {
+    "G": ("sbuf", [128, 4096], "bfloat16"), "BKI": ("sbuf", [128, 1024], "int32"),
+    "BK": ("sbuf", [128, 1152], "float32"), "IM": ("sbuf", [128, 1152], "bfloat16"),
+    "ZB": ("sbuf", [128, 256], "bfloat16"), "WI": ("sbuf", [128, 1], "int32"),
+    "Z1": ("sbuf", [128, 128], "bfloat16"), "Z2": ("sbuf", [128, 128], "bfloat16"),
+    "Z3": ("sbuf", [128, 128], "bfloat16"), "Z4": ("sbuf", [128, 128], "bfloat16"),
+    "CR": ("sbuf", [128, 384], "bfloat16"), "HI": ("sbuf", [128, 640], "bfloat16"), "TI": ("sbuf", [128, 640], "bfloat16"),
+    "X0": ("sbuf", [128, 8 * XS], "bfloat16"), "X1": ("sbuf", [128, 8 * XS], "bfloat16"),
+    "AB": ("sbuf", [128, 2048], "bfloat16"), "EQ": ("sbuf", [128, 1024], "bfloat16"),
+    "SEL": ("sbuf", [128, 512], "bfloat16"), "TRI": ("sbuf", [128, 512], "bfloat16"),
+    "cI": ("sbuf", [128, 128], "int32"), "cg": ("sbuf", [128, 640], "int32"), "cm": ("sbuf", [128, 128], "int32"),
+    "pc": ("sbuf", [128, 32], "int32"), "pf": ("sbuf", [128, 64], "float32"),
+    "tf": ("sbuf", [128, 128], "float32"), "tf2": ("sbuf", [128, 128], "float32"),
+    "rows": ("sbuf", [128, 1024], "bfloat16"),
+    "oXA": ("sbuf", [128, 16], "uint16"),
+    "P0": ("psum", [128, 512], "float32"), "P1": ("psum", [128, 512], "float32"), "P2": ("psum", [128, 512], "float32"),
+    "P3": ("psum", [128, 512], "float32"), "P4": ("psum", [128, 512], "float32"), "P5": ("psum", [128, 512], "float32"),
+    "P6": ("psum", [128, 512], "float32"), "P7": ("psum", [128, 512], "float32"),
+}
+for _n in ("I", "nI", "BO", "cap", "KF", "KC", "ONES", "HALF", "I16", "nI16", "nI256", "D32", "RS", "Kc", "Kn", "CO1", "CO2",
+           "WH", "WL", "VH", "VL",
+           "zT0", "zT1", "BE", "BD", "DM", "qt", "ivm", "Fs", "Sg", "W", "E1", "wq", "S", "nim"):
+    SCRATCH[_n] = ("sbuf", [128, 128], "bfloat16")
+for _n in ("R8", "G16", "hv"):
+    SCRATCH[_n] = ("sbuf", [128, 8], "bfloat16")
+for _n in ("Ui", "u", "sq", "s5", "bb", "bbm", "ub", "ubm", "bi", "bm"):
+    SCRATCH[_n] = ("sbuf", [128, 128], "int32")
+for _n in ("mb", "sw0", "sw1", "a", "c", "b", "h1", "h2", "h3", "hb1", "hb2", "e2", "s3", "t1", "nb"):
+    SCRATCH[_n] = ("sbuf", [128, 128], "float32")
+for _n in ("goff0", "goff1", "soff0", "soff1"):
+    SCRATCH[_n] = ("sbuf", [128, 8], "uint16")
+SCRATCH["b16"] = ("sbuf", [128, 128], "uint16")
+for _n in ("vi", "so"):
+    SCRATCH[_n] = ("sbuf", [128, 8], "int32")
+SCRATCH["vm"] = ("sbuf", [128, 16], "int32")
+for _n in ("nwi0", "nwi1", "dmin", "hm", "sk", "Ts"):
+    SCRATCH[_n] = ("sbuf", [128, 8], "float32")
+for _n in ("MK", "BT0", "BT1", "WE", "A12", "F", "FD", "C", "CD", "L"):
+    SCRATCH[_n] = ("sbuf", [128, 256], "bfloat16")
+for _n in ("Ps", "Ns"):
+    SCRATCH[_n] = ("sbuf", [128, 384], "bfloat16")
+SCRATCH["B"] = ("sbuf", [128, 128], "bfloat16")
+SCRATCH["SM"] = ("sbuf", [128, 128], "bfloat16")
+SCRATCH["XT"] = ("sbuf", [128, 128], "bfloat16")
+
+SEMAPHORES = ["sv", "sa", "st", "sg", "ls"] + ["dm%d" % i for i in range(8)] + ["rz%d" % t for t in range(1, 5)]
+CNT = {"v": "sv", "a": "sa", "t": "st", "g": "sg"}
+
+
+def build(g, T, topo, core):
+    ops = []
+
+    def op(q, dur, reads, writes, *fns, banks=(), sem=None):
+        ops.append({"q": q, "dur": dur, "r": tuple(reads), "w": tuple(writes), "f": fns, "b": tuple(banks), "sem": sem})
+
+    V, S, PE = g.vector, g.scalar, g.tensor
+
+    def dv(n, x=1.0):
+        return 35 + max(64.0, n * x) * 0.83 * 1.2
+
+    def ac(n):
+        return 60 + max(64.0, n) * 0.83 * 1.2
+
+    def pe(n):
+        return 60 + n * 0.6
+
+    def copy(out, in_, n, r, w, banks=(), x=1.0):
+        op("v", dv(n, x), r, w, lambda: V.tensor_copy(out, in_), banks=banks)
+
+    def tt(out, in0, in1, o, n, r, w, banks=(), x=2.0):
+        op("v", dv(n, x), r, w, lambda: V.tensor_tensor(out, in0, in1, o), banks=banks)
+
+    def ts(out, in0, s1, o1, n, r, w, s2=None, o2=None, banks=(), x=1.0):
+        if o2 is None:
+            op("v", dv(n, x), r, w, lambda: V.tensor_scalar(out, in0, s1, None, o1), banks=banks)
+        else:
+            op("v", dv(n, x), r, w, lambda: V.tensor_scalar(out, in0, s1, s2, o1, o2), banks=banks)
+
+    def scan(out, d0, d1, o0, o1, n, r, w, banks=()):
+        op("v", dv(n), r, w, lambda: V.tensor_tensor_scan(out, d0, d1, 0.0, o0, o1), banks=banks)
+
+    def act(out, in_, f, n, r, w, bias=0.0, scale=1.0, banks=(), x=1.0):
+        op("a", ac(n * x), r, w, lambda: S.activation(out, in_, f, bias, scale), banks=banks)
+
+    def mm(n, r, bank, *calls, grp=(), hard=False):
+        def one(a):
+            return lambda: PE.matmul(*a)
+        op("t", pe(n), r, grp, *[one(a) for a in calls], banks=(bank,))
+        ops[-1]["hard"] = hard
+
+    def memset(ap, val, n, w):
+        op("v", dv(n, 0.5), (), w, lambda: V.memset(ap, val))
+
+    nd = [0]
+
+    def load(out, in_, w, dur, r=()):
+        s = "dm%d" % nd[0]
+        nd[0] += 1
+        op("s", dur, r, w, lambda: g.sync.dma_start(out, in_), sem=(s, 16))
+
+    load(T.WI[:], T.wt[:], ("WI",), 2000)
+    load(T.ZB[:], T.bites[:], ("ZB",), 2200)
+    load(T.BKI[:], T.bank[:], ("BKI",), 4000)
+    load(T.IM[:, 0:1024], T.immun[:], ("IM",), 5000)
+    load(T.G[:], T.geno[:], ("G",), 8500)
+
+    rank = T.rank_of(core)
+    cores = list(T.cores)
+    nr = len(cores)
+
+    def engs(src, dst):
+        return topo.engines(src, dst)[:8]
+
+    def send(src_ap, key, dst, t):
+        e = engs(core, dst)
+        m = 0
+        for x in e:
+            m |= 1 << x
+        a = topo.addr(dst)
+        zt = T["Z%d" % t]
+        op("g", 300, (key,), ("sent%d" % t,), lambda: g.remote_dma(zt[:], src_ap, T.sem["rz%d" % t], T.sem.ls, a[1], a[0], m),
+           sem=("ls", len(e)))
+        frm = cores[(rank - (1 if t == 1 else 2)) % nr]
+        op("n", 3500, ("sent%d" % t,), ("Z%d" % t,), sem=("rz%d" % t, len(engs(frm, core))))
+
+    op("g", 180, (), ("pI",), lambda: g.iota(T.pc[:, 0:1], [[1, 1]], 0, 1))
+    op("g", 380, (), ("cg",), lambda: g.iota(T.cg[:, 0:128], [[1, 8], [0, 16]], 0, 0))
+    op("g", 380, (), ("cm",), lambda: g.iota(T.cm[:], [[0, 8], [1, 16]], 0, 0))
+    op("g", 380, (), ("cI",), lambda: g.iota(T.cI[:], [[1, 128]], 0, 0))
+    memset(T.ONES[:], 1.0, 128, ("ONES",))
+    memset(T.HALF[:], 0.5, 128, ("HALF",))
+    memset(T.rows[:, 0:128], -2080.0, 128, ("rowA",))
+    memset(T.rows[:, 128:256], 2336.0, 128, ("rowB",))
+    memset(T.TRI[:], -10.0, 512, ("TRI",))
+    memset(T.c[:], 0.0, 128, ("c",))
+    for n in ("h1", "h2", "h3"):
+        memset(T[n][:], 0.0, 128, (n,))
+    op("g", 1000, ("TRI",), ("TRI",), lambda: g.affine_select(T.TRI[:], T.TRI[:], [[0, 4], [-1, 128]], OP.is_ge, 0.0, 0, 1))
+    pc, pf = T.pc, T.pf
+    pi = pc[:, 0:1]
+    copy(pf[:, 0:1], pi, 1, ("pI",), ("f0",))
+    ts(pc[:, 1:2], pi, 4, OP.logical_shift_right, 1, ("pI",), ("i1",))
+    ts(pc[:, 2:3], pi, 15, OP.bitwise_and, 1, ("pI",), ("i2",))
+    copy(pf[:, 1:2], pc[:, 1:2], 1, ("i1",), ("f1",))
+    copy(pf[:, 2:3], pc[:, 2:3], 1, ("i2",), ("f2",))
+    cI = T.cI[:]
+    op("g", 1050, (), ("cg5",), lambda: g.iota(T.cg[:, 128:640], [[1, 32], [0, 16]], 0, 0))
+    cg, cm = T.cg[:, 0:128], T.cm[:]
+    ts(T.BO[:], cg, pf[:, 1:2], OP.is_equal, 128, ("cg", "f1"), ("BO",))
+    ts(pc[:, 8:9], T.WI[:], 4032, OP.bitwise_and, 1, ("WI",), ("i8",))
+    ts(pc[:, 9:10], T.WI[:], 63, OP.bitwise_and, 1, ("WI",), ("i9",))
+    copy(pf[:, 8:9], pc[:, 8:9], 1, ("i8",), ("f8",))
+    copy(pf[:, 9:10], pc[:, 9:10], 1, ("i9",), ("f9",))
+    ts(T.WH[:], T.BO[:], pf[:, 8:9], OP.mult, 128, ("BO", "f8"), ("WH",))
+    ts(T.WL[:], T.BO[:], pf[:, 9:10], OP.mult, 128, ("BO", "f9"), ("WL",))
+    ts(pc[:, 10:11], T.WI[:], 37, OP.mult, 1, ("WI",), ("i10",))
+    ts(pc[:, 11:12], pc[:, 10:11], 992, OP.bitwise_and, 1, ("i10",), ("i11",))
+    ts(pc[:, 12:13], pc[:, 10:11], 31, OP.bitwise_and, 1, ("i10",), ("i12",))
+    copy(pf[:, 11:12], pc[:, 11:12], 1, ("i11",), ("f11",))
+    copy(pf[:, 12:13], pc[:, 12:13], 1, ("i12",), ("f12",))
+    ts(T.VH[:], T.BO[:], pf[:, 11:12], OP.mult, 128, ("BO", "f11"), ("VH",))
+    ts(T.VL[:], T.BO[:], pf[:, 12:13], OP.mult, 128, ("BO", "f12"), ("VL",))
+    ts(T.MK[:, 0:128], cm, pf[:, 2:3], OP.is_equal, 128, ("cm", "f2"), ("MKa",))
+    copy(T.MK[:, 128:256], T.MK[:, 0:128], 128, ("MKa",), ("MK",), x=0.5)
+    ts(T.RS[:], cm, 0.0, OP.is_gt, 128, ("cm",), ("RS",))
+    ts(T.I[:], cI, pf[:, 0:1], OP.is_equal, 128, ("cI", "f0"), ("I",))
+    ts(T.R8[:], T.cI[:, 0:8], pf[:, 1:2], OP.is_equal, 8, ("cI", "f1"), ("R8",))
+    ts(T.tf[:], T.RS[:], 0.5, OP.mult, 128, ("RS",), ("tf",))
+    ts(T.tf2[:], T.RS[:], -512.0, OP.mult, 128, ("RS",), ("tf2",), s2=512.0, o2=OP.add)
+    scan(T.mb[:], T.tf[:], T.tf2[:], OP.mult, OP.add, 128, ("tf", "tf2"), ("mb",))
+    tt(T.tf[:], T.mb[:], T.I[:], OP.mult, 128, ("mb", "I"), ("tf",))
+    op("v", dv(128), ("tf",), ("f5",), lambda: V.tensor_reduce(pf[:, 5:6], T.tf[:], AxisListType.X, OP.add))
+    ts(pf[:, 6:7], pf[:, 2:3], 8.0, OP.is_ge, 1, ("f2",), ("f6",))
+    ts(pf[:, 7:8], pf[:, 6:7], 63.75, OP.mult, 1, ("f6",), ("f7",), s2=0.25, o2=OP.add)
+    tt(pf[:, 10:11], pf[:, 7:8], pf[:, 5:6], OP.mult, 1, ("f7", "f5"), ("f10",))
+    ts(pc[:, 13:14], pc[:, 1:2], 1, OP.bitwise_and, 1, ("i1",), ("i13",))
+    ts(pf[:, 13:14], pf[:, 2:3], 10.0, OP.is_lt, 1, ("f2",), ("f13",))
+    tt(pf[:, 14:15], pf[:, 13:14], pc[:, 13:14], OP.mult, 1, ("f13", "i13"), ("f14",))
+    tt(pf[:, 15:16], pf[:, 13:14], pf[:, 14:15], OP.subtract, 1, ("f13", "f14"), ("f15",))
+    ts(pf[:, 16:18], pf[:, 14:16], 1.0 / 256, OP.mult, 2, ("f14", "f15"), ("f16",))
+    ts(pf[:, 18:20], pf[:, 14:16], -1.0, OP.mult, 2, ("f14", "f15"), ("f18",))
+    ts(T.tf[:, 0:8], T.cI[:, 0:8], 16.0, OP.mult, 8, ("cI", "tf"), ("tf",), s2=1024.0, o2=OP.add)
+    ts(pf[:, 48:56], T.tf[:, 0:8], pf[:, 2:3], OP.add, 8, ("tf", "f2"), ("iw",))
+    copy(T.BK[:, 0:1024], T.BKI[:], 1024, ("BKI",), ("BK",))
+    ts(pc[:, 3:4], pi, 31, OP.bitwise_and, 1, ("pI",), ("i3",))
+    copy(pf[:, 3:4], pc[:, 3:4], 1, ("i3",), ("f3",))
+    ts(pf[:, 4:5], pf[:, 0:1], 32.0, OP.mult, 1, ("f0",), ("f4",))
+    ts(T.SEL[:], T.cg[:, 128:640], pf[:, 3:4], OP.is_equal, 512, ("cg5", "f3"), ("SEL",), s2=-1.0, o2=OP.mult)
+    ts(T.G16[:], T.R8[:], 16.0, OP.mult, 8, ("R8",), ("G16",))
+    act(T.KC[:], T.BO[:], AF.Copy, 128, ("BO",), ("KC",), scale=128.0)
+    ts(T.rows[:, 512:640], cm, -1.0, OP.mult, 128, ("cm",), ("rowR",), s2=15.0, o2=OP.add)
+    ts(T.rows[:, 672:688], T.cI[:, 0:16], 8.0, OP.is_ge, 16, ("cI",), ("rowZ",), s2=-8.0, o2=OP.mult)
+    tt(T.rows[:, 656:672], T.cI[:, 0:16], T.rows[:, 672:688], OP.add, 16, ("cI", "rowZ"), ("rowY",))
+    ts(T.rows[:, 640:656], T.rows[:, 656:672], 256.0, OP.mult, 16, ("rowY",), ("rowX",))
+
+    def cst(name, t):
+        return T[name][:, 128 * t:128 * t + 128]
+
+    def scaled(name, val, t=None):
+        out = T[name][:] if t is None else cst(name, t)
+        act(out, T.I[:], AF.Copy, 128, ("I",), (name if t is None else name + str(t),), scale=val)
+
+    for name, val in (("KF", THR), ("I16", 16.0), ("nI16", -16.0), ("nI", -1.0), ("nI256", -256.0)):
+        scaled(name, val)
+    ts(T.D32[:], T.I[:], pf[:, 4:5], OP.mult, 128, ("I", "f4"), ("D32",), x=0.5)
+    for t in range(NST):
+        scaled("HI", 4096.0 * (8 + t), t)
+        if t:
+            scaled("TI", float(t), t)
+    for j in range(2):
+        memset(T["X%d" % j][:, ::XS], -1.0, 8, ["Xs%d" % j])
+    ts(pf[:, 20:21], pf[:, 2:3], 1.0, OP.add, 1, ("f2",), ("f20",))
+    ts(T.tf2[:], cm, 16.0, OP.mult, 128, ("cm", "f20"), ("tf2",), s2=pf[:, 20:21], o2=OP.add)
+    tt(T.Kc[:], T.tf2[:], T.BO[:], OP.mult, 128, ("tf2", "BO"), ("Kc",))
+    ts(T.Kn[:], T.Kc[:], -1.0, OP.mult, 128, ("Kc",), ("Kn",), x=0.5)
+    ts(pc[:, 4:5], pi, 3, OP.logical_shift_right, 1, ("pI",), ("i4",))
+    ts(pc[:, 5:6], pi, 7, OP.bitwise_and, 1, ("pI",), ("i5",))
+    copy(pf[:, 21:22], pc[:, 5:6], 1, ("i5",), ("f21",))
+    for j in range(6):
+        ts(pf[:, 22 + j:23 + j], pc[:, 4:5], float(j), OP.is_equal, 1, ("i4",), ("f%d" % (22 + j),))
+    tt(pf[:, 32:35], pf[:, 22:25], pf[:, 25:28], OP.add, 3, ["f%d" % j for j in range(22, 28)], ("f32",))
+    tt(pf[:, 35:37], pf[:, 32:34], pf[:, 33:35], OP.subtract, 2, ("f32",), ("f35",))
+    tt(pf[:, 37:38], pf[:, 32:33], pf[:, 34:35], OP.subtract, 1, ("f32",), ("f37",))
+    for j in range(3):
+        ts(T.SM[:, 8 * j:8 * j + 8], T.cI[:, 0:8], pf[:, 21:22], OP.is_equal, 8, ("cI", "f21", "f35", "f37"), ("M1%d" % j,),
+           s2=pf[:, 35 + j:36 + j], o2=OP.mult)
+    memset(T.SM[:, 24:32], 0.0, 8, ("M13",))
+    memset(T.SM[:, 32:120], 0.0, 88, ("RB",))
+    copy(T.SM[:, 72:80], T.R8[:], 8, ("R8",), ("RB",), x=0.5)
+    ts(pf[:, 38:44], pf[:, 22:28], 0.5, OP.mult, 6, ["f%d" % j for j in range(22, 28)], ("f38",))
+    ts(pf[:, 29:30], pf[:, 26:27], -4.0, OP.mult, 1, ("f26",), ("f29",))
+    tt(pf[:, 44:45], pf[:, 39:40], pf[:, 38:39], OP.subtract, 1, ("f38",), ("f44",))
+    tt(pf[:, 28:29], pf[:, 44:45], pf[:, 29:30], OP.add, 1, ("f44", "f29"), ("f28",))
+    tt(pf[:, 45:46], pf[:, 39:40], pf[:, 40:41], OP.add, 1, ("f38",), ("f45",))
+    tt(pf[:, 30:31], pf[:, 29:30], pf[:, 45:46], OP.subtract, 1, ("f29", "f45"), ("f30",))
+    ts(T.CO1[:], cg, pf[:, 21:22], OP.is_equal, 128, ("cg", "f21", "f28"), ("CO1",), s2=pf[:, 28:29], o2=OP.mult)
+    ts(T.CO2[:], cg, pf[:, 21:22], OP.is_equal, 128, ("cg", "f21", "f30"), ("CO2",), s2=pf[:, 30:31], o2=OP.mult)
+
+    P0, P1, P2, P3, P4, P5, P6, P7 = [T["P%d" % i] for i in range(8)]
+    one1 = T.ONES[0:1, :]
+
+    def zap(t):
+        return T.ZB[:, 0:128] if t == 0 else T["Z%d" % t][:]
+
+    def zk(t):
+        return "ZB" if t == 0 else "Z%d" % t
+
+    def prep(t):
+        z, k, d = zap(t), zk(t), t % 2
+        mm(256, (k, "WH", "WL"), "P6", (P6[:, 0:128], T.WH[:], z, True, False), (P6[:, 0:128], T.WL[:], z, False, True))
+        mm(256, (k, "VH", "VL"), "P6", (P6[:, 128:256], T.VH[:], z, True, False), (P6[:, 128:256], T.VL[:], z, False, True))
+        copy(T.Ui[:], P6[:, 0:128], 128, (), ("Ui",), banks=("P6",))
+        ts(T.u[:], T.Ui[:], 4095, OP.bitwise_and, 128, ("Ui",), ("u",))
+        tt(T.sq[:], T.u[:], T.u[:], OP.mult, 128, ("u",), ("sq",))
+        ts(T.s5[:], T.sq[:], 5, OP.logical_shift_right, 128, ("sq",), ("s5",))
+        tt(P6[:, 256:384], T.s5[:], P6[:, 128:256], OP.add, 128, ("s5",), ("base",), banks=("P6",), x=1.0)
+        sw = T["sw%d" % d]
+        tt(T.mb[:], P6[:, 256:384], T.MK[:, 0:128], OP.mult, 128, ("base", "MKa"), ("mb",), banks=("P6",), x=1.0)
+        scan(sw[:], T.RS[:], T.mb[:], OP.mult, OP.add, 128, ("RS", "mb"), ("sw%d" % d,))
+        mm(128, (k, "I"), "P6", (P6[:, 384:512], z, T.I[:], True, True))
+        act(T["zT%d" % d][:], P6[:, 384:512], AF.Copy, 128, (), ("zT%d" % d,), banks=("P6",))
+
+    def dups(t):
+        z, k, d = zap(t), zk(t), t % 2
+        ts(T.bb[:], P6[:, 256:384], pf[:, 5:6], OP.mult, 128, ("base", "f5"), ("bb",), banks=("P6",))
+        if t <= NST - 3:
+            ts(T.ub[:], P6[:, 0:128], pf[:, 10:11], OP.mult, 128, ("f10",), ("ub",), banks=("P6",))
+            ts(T.ubm[:], T.ub[:], 128, OP.bitwise_and, 128, ("ub",), ("ubm",))
+            bt = T["BT%d" % d]
+            ts(bt[:, 0:128], T.ubm[:], -1.0 / 128, OP.mult, 128, ("ubm",), ("bta%d" % d,))
+            copy(bt[:, 128:256], bt[:, 0:128], 128, ("bta%d" % d,), ("BT%d" % d,), x=0.5)
+        ts(T.bbm[:], T.bb[:], 512, OP.bitwise_and, 128, ("bb",), ("bbm",))
+        ts(T.BD[:], T.bbm[:], pf[:, 16:17], OP.mult, 128, ("bbm", "f16", "f18"), ("BD",), s2=pf[:, 18:19], o2=OP.add)
+        ts(T.BE[:], T.bbm[:], pf[:, 17:18], OP.mult, 128, ("bbm", "f16", "f18"), ("BE",), s2=pf[:, 19:20], o2=OP.add)
+        for h in range(2):
+            for j in range(2):
+                calls = [] if j else [(P0[:, 0:512], T.I[:], T.TRI[:], True, False)]
+                for i in range(2):
+                    bx = (T.BD if i else T.BE)[64 * h + 32 * j:64 * h + 32 * j + 32, :]
+                    calls.append((P0[:, 256 * j + 128 * i:256 * j + 128 * i + 128], bx, bx, False, j + i == 2))
+                mm(256 if j else 768, ("I", "TRI", "BD", "BE"), "P0", *calls, grp=("gdup",), hard=bool(j))
+            act(T.EQ[:, 512 * h:512 * h + 512], P0[:], AF.Relu, 512, (), ("EQ%d" % h,), bias=-9.0, banks=("P0",))
+        mm(512, ("EQ0", "EQ1", "ONES"), "P6",
+           *[(P6[:, 16 * j:16 * j + 16], T.EQ[:, 128 * j:128 * j + 128], T.ONES[:, 0:16], True, True) for j in range(8)])
+        tt(T.DM[:], P6[:, 0:128], T.MK[:, 0:128], OP.mult, 128, ("MKa",), ("DM",), banks=("P6",), x=1.0)
+        mm(64, ("DM", "R8"), "P6", (P6[:, 128:136], T.DM[:], T.R8[:], True, True))
+        ts(T.dmin[:], P6[:, 128:136], 1.0, OP.min, 8, (), ("dmin",), banks=("P6",))
+        tt(T["nwi%d" % d][:], T.dmin[:], pf[:, 48:56], OP.mult, 8, ("dmin", "iw"), ("nwi%d" % d,))
+
+    def voff(t):
+        d = t % 2
+        if t == 0:
+            copy(T.vi[:], T.sw0[:, 15::16], 8, ("sw0",), ("vi",))
+        else:
+            ts(T.vi[:], T["sw%d" % d][:, 15::16], pf[:, 63:64], OP.add, 8, ("sw%d" % d, "A"), ("vi",))
+        ts(T.vm[:, 8 * d:8 * d + 8], T.vi[:], 1023, OP.bitwise_and, 8, ("vi",), ("vm%d" % d,))
+        copy(T["goff%d" % d][:], T.vm[:, 8 * d:8 * d + 8], 8, ("vm%d" % d,), ("goff%d" % d,))
+
+    def soff(t):
+        d = t % 2
+        tt(T.so[:], T.vm[:, 8 * d:8 * d + 8], T["nwi%d" % d][:], OP.max, 8, ("vm%d" % d, "nwi%d" % d), ("so",))
+        copy(T["soff%d" % d][:], T.so[:], 8, ("so",), ("soff%d" % d,))
+
+    def main(t):
+        d = t % 2
+        z, k = zap(t), zk(t)
+        last = t == NST - 1
+        go, gk = T["goff%d" % d][:, 0:8], "goff%d" % d
+        X, xk = T["X%d" % d], "X%d" % d
+        win = T.BK[:, 0:1024]
+        copy(T.bi[:], win.indirect(go), 128, ("BK", gk), ("bi",), x=1.6)
+        act(T.qt[:], win.indirect(go), AF.Identity, 128, ("BK", gk), ("qt",), bias=129.5 + 2.0 ** -14, scale=1.0 / 4096, x=1.6)
+        ts(T.bm[:], T.bi[:], 4095, OP.bitwise_and, 128, ("bi",), ("bm",))
+        copy(T.b16[:], T.bm[:], 128, ("bm",), ("b16",))
+        act(T.Fs[:], T.qt[:], AF.Sign, 128, ("qt",), ("Fs",), bias=-(131.5 + t))
+        for c in range(8):
+            off = T.b16[:, 16 * c:16 * c + 16]
+            out = X[:, XS * c + 1:XS * c + 257]
+            if c in ON_DVE:
+                copy(out, T.G[:].indirect(off), 256, ("G", "b16"), (xk + str(c),), x=1.6)
+            else:
+                act(out, T.G[:].indirect(off), AF.Copy, 256, ("G", "b16"), (xk + str(c),), x=1.6)
+        act(T.ivm[:], T.IM[:, 0:1024].indirect(go), AF.Identity, 128, ("IM", gk), ("ivm",), bias=-1.0, x=1.6)
+        mm(256, (k, "ivm", "I", "nI"), "P7", (P7[:, 0:128], T.I[:], z, True, False), (P7[:, 0:128], T.nI[:], T.ivm[:], False, True))
+        act(T.Sg[:], P7[:, 0:128], AF.Sign, 128, (), ("Sg",), bias=-1.5, banks=("P7",))
+        mm(256, ("qt", "I16", "ONES", "rowA"), "P7", (P7[:, 128:256], one1, T.rows[0:1, 0:128], True, False),
+           (P7[:, 128:256], T.qt[:], T.I16[:], False, True))
+        mm(384, ("qt", "nI16", "ONES", "rowB", "rowR"), "P7", (P7[:, 256:384], one1, T.rows[0:1, 128:256], True, False),
+           (P7[:, 256:384], one1, T.rows[0:1, 512:640], False, False), (P7[:, 256:384], T.qt[:], T.nI16[:], False, True))
+        mm(256, ("Fs", "KF", "rowR", "ONES"), "P5", (P5[:, 0:128], one1, T.rows[0:1, 512:640], True, False),
+           (P5[:, 0:128], T.Fs[:], T.KF[:], False, False), grp=("gkey",))
+        for e in range(4):
+            bank = "P%d" % (1 + e % 2)
+            pb = T[bank]
+            zt = T["zT%d" % d][32 * e:32 * e + 32, :]
+            mm(512, ("zT%d" % d, "SEL"), bank, (pb[:], zt, T.SEL[32 * e:32 * e + 32, :], True, False), grp=("g" + bank,))
+            for j in range(2):
+                c = 2 * e + j
+                mm(256, (xk + str(c), "I"), bank, (pb[:, 256 * j:256 * j + 256], T.I[:], X[:, XS * c + 1:XS * c + 257], False, j == 1), grp=("g" + bank,))
+            act(T.AB[:, 512 * e:512 * e + 512], pb[:], AF.Abs, 512, (), ("AB%d" % e,), banks=(bank,))
+            if e == 2:
+                mm(1024, ("AB0", "AB1", "AB2", "G16"), "P5",
+                   *[(P5[0:96, kk:128:16], T.AB[:, kk:1536:16], T.G16[:], False, kk == 15) for kk in range(16)], grp=("gkey",))
+            if e == 3:
+                mm(512, ("AB3", "G16"), "P5",
+                   *[(P5[96:128, kk:128:16], T.AB[:, 1536 + kk:2048:16], T.G16[:], False, kk == 15) for kk in range(16)], grp=("gkey",))
+        dups(t)
+        soff(t)
+        copy(T.G[:, t::32], z, 128, (k,), ("G",), x=0.5)
+        mm(192, ("Sg", "KC", "R8"), "P7", (P7[:, 0:128], T.Sg[:], T.KC[:], True, True), (P7[:, 392:400], T.Sg[:], T.R8[:], True, True))
+        act(T.cap[:], P7[:, 0:128], AF.Relu, 128, (), ("cap",), banks=("P7",))
+        ts(T.sk[:], P7[:, 392:400], 1.0, OP.is_ge, 8, (), ("sk",), banks=("P7",))
+        tt(P7[:, 128:256], P7[:, 128:256], T.cap[:], OP.min, 128, ("cap",), ("q16s",), banks=("P7",), x=1.0)
+        ts(T.Ts[:], T.sk[:], -BIG, OP.mult, 8, ("sk",), ("Ts",), s2=BIG + THR, o2=OP.add)
+        if last:
+            load(T.ygeno[:], T.G[:], ("yg",), 7000, r=("G",))
+        else:
+            mm(64, ("Fs", "R8"), "P7", (P7[:, 384:392], T.Fs[:], T.R8[:], True, True))
+            ts(T.hm[:], P7[:, 384:392], -12.0, OP.min, 8, (), ("hm",), s2=16.0, o2=OP.add, banks=("P7",))
+            tt(T.hv[:], T.hm[:], T.sk[:], OP.mult, 8, ("hm", "sk"), ("hv",))
+            mm(64, ("hv", "HALF"), "P7", (P7[:, 400:408], T.HALF[:], T.hv[:], True, True))
+            op("v", dv(8), (), ("A",), lambda: V.tensor_reduce(pf[:, 63:64], P7[:, 400:408], AxisListType.X, OP.add), banks=("P7",))
+            prep(t + 1)
+            voff(t + 1)
+        key = P5[:, 0:128]
+        scan(T.a[:], T.RS[:], key, OP.mult, OP.max, 128, ("RS",), ("a",), banks=("P5",))
+        tt(T.c[:, 1:128], T.a[:, 0:127], P5[:, 1:128], OP.min, 128, ("a",), ("c",), banks=("P5",), x=1.0)
+        scan(T.b[:], T.c[:], T.RS[:], OP.max, OP.mult, 128, ("c", "RS"), ("b",))
+        ts(T.h2[:, 0::16], T.b[:, 15::16], THR, OP.max, 8, ("b",), ("h2",))
+        scan(T.hb2[:], T.RS[:], T.h2[:], OP.mult, OP.add, 128, ("h2", "RS"), ("hb2",))
+        tt(T.W[:], key, T.hb2[:], OP.is_ge, 128, ("hb2",), ("W",), banks=("P5",), x=1.0)
+        tt(T.wq[:], P7[:, 128:256], T.W[:], OP.mult, 128, ("W", "q16s"), ("wq",), banks=("P7",), x=1.0)
+        tt(T.e2[:], P7[:, 256:384], T.wq[:], OP.add, 128, ("wq",), ("e2",), banks=("P7",), x=1.0)
+        scan(T.s3[:], T.RS[:], T.e2[:], OP.mult, OP.max, 128, ("e2", "RS"), ("s3",))
+        copy(T.h3[:, 0::16], T.s3[:, 15::16], 8, ("s3",), ("h3",))
+        scan(P5[:, 384:512], T.RS[:], T.h3[:], OP.mult, OP.add, 128, ("h3", "RS"), ("hb3",), banks=("P5",))
+        tt(T.S[:], T.e2[:], P5[:, 384:512], OP.is_equal, 128, ("e2", "hb3"), ("S",), banks=("P5",), x=1.0)
+        ts(T.h1[:, 0::16], T.a[:, 15::16], THR, OP.max, 8, ("a",), ("h1",))
+        scan(T.hb1[:], T.RS[:], T.h1[:], OP.mult, OP.add, 128, ("h1", "RS"), ("hb1",))
+        tt(T.E1[:], key, T.hb1[:], OP.is_ge, 128, ("hb1",), ("E1",), banks=("P5",), x=1.0)
+        tt(T.SM[:, 120:128], T.a[:, 15::16], T.Ts[:], OP.is_ge, 8, ("a", "Ts"), ("XBh",))
+        mm(128, ("wq", "nI256"), "P7", (P7[:, 0:128], T.wq[:], T.nI256[:], True, True))
+        calls = [(P5[:, 256:384], T.S[:], T.D32[:], True, False)]
+        if t:
+            calls.append((P5[:, 256:384], T.S[:], cst("TI", t), False, False))
+        calls.append((P5[:, 256:384], T.S[:], cst("HI", t), False, True))
+        tt(T.t1[:], T.bi[:], P7[:, 0:128], OP.add, 128, ("bi",), ("t1",), banks=("P7",), x=1.0)
+        mm(384, ("S", "D32", "HI%d" % t) + (("TI%d" % t,) if t else ()), "P5", *calls)
+        tt(T.nb[:], T.t1[:], P5[:, 256:384], OP.max, 128, ("t1",), ("nb",), banks=("P5",), x=1.0)
+        so, sk_ = T["soff%d" % d][:, 0:8], "soff%d" % d
+        copy(T.BK[:, 0:1152].indirect(so), T.nb[:], 128, ("nb", sk_), ("BK",), x=3.5)
+        if last:
+            load(T.ybank[:], T.BK[:, 0:1024], ("yb",), 4000, r=("BK",))
+        mm(256, ("W", "E1", "I"), "P3", (P3[:, 0:128], T.E1[:], T.I[:], True, True), (P3[:, 128:256], T.W[:], T.I[:], True, True))
+        act(T.WE[:], P3[:, 0:256], AF.Copy, 256, (), ("WE",), banks=("P3",))
+        mm(384, ("WE", "Kc", "Kn"), "P3", (P3[:, 256:384], T.WE[:, 0:128], T.Kc[:], True, True),
+           (P3[:, 384:512], T.WE[:, 128:256], T.Kc[:], True, False), (P3[:, 384:512], T.WE[:, 0:128], T.Kn[:], False, True))
+        tt(T.L[:], P3[:, 256:512], T.MK[:], OP.mult, 256, ("MK",), ("L",), banks=("P3",), x=1.0)
+        mm(256, ("L", "R8", "ONES", "rowX", "rowY"), "P3", (P3[:, 0:16], one1, T.rows[0:1, 640:656], True, False),
+           (P3[:, 0:16], one1, T.rows[0:1, 656:672], False, False),
+           (P3[:, 0:8], T.L[:, 0:128], T.R8[:], False, False), (P3[:, 8:16], T.L[:, 128:256], T.R8[:], False, True))
+        copy(T.oXA[:], P3[:, 0:16], 16, (), ("oXA",), banks=("P3",))
+        act(T.A12[:], X[:].indirect(T.oXA[:, 0:16]), AF.Copy, 256, ["oXA", "Xs%d" % d] + [xk + str(c) for c in range(8)], ("A12",), x=1.6)
+        for j in range(2):
+            mm(256, ("A12", k, "I", "nI"), "P4", (P4[:, 128 * j:128 * j + 128], T.nI[:], z, True, False),
+               (P4[:, 128 * j:128 * j + 128], T.I[:], T.A12[:, 128 * j:128 * j + 128], False, True))
+        mm(256, ("A12", "I", "nI"), "P4", (P4[:, 256:384], T.I[:], T.A12[:, 128:256], True, False),
+           (P4[:, 256:384], T.nI[:], T.A12[:, 0:128], False, True))
+        act(T.Ps[:], P4[:, 0:384], AF.Sign, 384, (), ("Ps",), bias=-0.5, banks=("P4",))
+        act(T.Ns[:], P4[:, 0:384], AF.Sign, 384, (), ("Ns",), bias=-0.5, scale=-1.0, banks=("P4",))
+
+        def cnt(j, buf, i, first=False, last_=False):
+            return (P4[0:48, 384:512], T.SM[:, 72 - 8 * j:120 - 8 * j], buf[:, 128 * i:128 * i + 128], first, last_)
+        mm(384, ("Ps", "RB"), "P4", cnt(0, T.Ps, 0, True), cnt(3, T.Ps, 1), cnt(4, T.Ps, 2), grp=("gcnt",))
+        mm(384, ("Ns", "RB"), "P4", cnt(1, T.Ns, 0), cnt(2, T.Ns, 1), cnt(5, T.Ns, 2, False, True), grp=("gcnt",))
+        act(T.B[0:48, :], P4[0:48, 384:512], AF.Sign, 128, (), ("B",), bias=-1.0, banks=("P4",))
+        mm(192, ("B", "M10", "M11", "M12", "M13", "XBh", "I"), "P3", (P3[0:32, 0:128], T.SM[0:48, 0:32], T.B[0:48, :], True, True),
+           (P3[32:40, 0:128], T.SM[:, 120:128], T.I[:], True, True))
+        act(T.XT[0:40, :], P3[0:40, 0:128], AF.Sign, 128, (), ("XT",), bias=-1.0, banks=("P3",))
+        mm(256, ("XT", "CO1", "CO2"), "P0", (P0[:, 0:128], T.CO1[0:40, :], T.XT[0:40, :], True, True),
+           (P0[:, 128:256], T.CO2[0:40, :], T.XT[0:40, :], True, True))
+        bt = "BT%d" % d
+        if t <= NST - 3:
+            tt(T.C[:], P0[:, 0:256], T[bt][:], OP.is_equal, 256, (bt,), ("C",), banks=("P0",), x=1.0)
+            tt(T.CD[:], T.C[:], P4[:, 0:256], OP.mult, 256, ("C",), ("CD",), banks=("P4",), x=1.0)
+        act(T.F[:], P0[:, 0:256], AF.Relu, 256, (), ("F",), scale=-1.0, banks=("P0",))
+        tt(T.FD[:], T.F[:], P4[:, 0:256], OP.mult, 256, ("F",), ("FD",), banks=("P4",), x=1.0)
+        mm(384, ("FD", k, "I"), "P0", (P0[:, 256:384], T.I[:], z, True, False), (P0[:, 256:384], T.I[:], T.FD[:, 0:128], False, False),
+           (P0[:, 256:384], T.I[:], T.FD[:, 128:256], False, True))
+        tt(T.nim[:], T.ivm[:], P0[:, 256:384], OP.max, 128, ("ivm",), ("nim",), banks=("P0",), x=1.0)
+        copy(T.IM[:, 0:1152].indirect(so), T.nim[:], 128, ("nim", sk_), ("IM",), x=3.5)
+        if last:
+            load(T.yimm[:], T.IM[:, 0:1024], ("yi",), 3500, r=("IM",))
+        if t <= NST - 3:
+            mm(384, ("CD", k, "I"), "P3", (P3[:, 256:384], T.I[:], z, True, False), (P3[:, 256:384], T.I[:], T.CD[:, 0:128], False, False),
+               (P3[:, 256:384], T.I[:], T.CD[:, 128:256], False, True))
+            cr = "CR%d" % t
+            act(cst("CR", t), P3[:, 256:384], AF.Copy, 128, (), (cr,), banks=("P3",))
+            send(cst("CR", t), cr, cores[(rank + 2) % nr], t + 2)
+
+    send(T.ZB[:, 128:256], "ZB", cores[(rank + 1) % nr], 1)
+    prep(0)
+    voff(0)
+    for t in range(NST):
+        main(t)
+    return ops
+
+
+def depend(ops):
+    lw, rd, bank, rdy, prev = {}, {}, {}, [], []
+    lastq = {}
+    for i, o in enumerate(ops):
+        need, order = set(), set()
+        for k in o["r"]:
+            if k in lw:
+                need |= lw[k]
+            rd.setdefault(k, []).append(i)
+        for k in o["w"]:
+            if k in lw:
+                need |= lw[k]
+            need |= set(rd.get(k, ()))
+        for k in o["w"]:
+            lw[k] = {i}
+            rd[k] = []
+        for k in o["b"]:
+            h = bank.setdefault(k, [None, set(), set()])
+            if h[0] != o["q"]:
+                h[0], h[1], h[2] = o["q"], h[2], set()
+            need |= h[1]
+            h[2].add(i)
+        if o["q"] in ("s", "g"):
+            if o["q"] in lastq:
+                order.add(lastq[o["q"]])
+            lastq[o["q"]] = i
+        need.discard(i)
+        order.discard(i)
+        rdy.append(need)
+        prev.append(order)
+    return rdy, prev
+
+
+def graph(ops, need, order):
+    n = len(ops)
+    nxt = [[] for _ in range(n)]
+    cnt = [0] * n
+    for i in range(n):
+        for j in sorted(need[i] | order[i]):
+            nxt[j].append((i, j not in need[i]))
+            cnt[i] += 1
+    base = [0.0] * n
+    for i in range(n - 1, -1, -1):
+        base[i] = ops[i]["dur"] + max([base[j] + 40 for j, _ in nxt[i]], default=0.0)
+    return [o["q"] for o in ops], [o["dur"] for o in ops], nxt, cnt, base
+
+
+def schedule(gr, off):
+    q, dur, nxt, cnt, base = gr
+    n = len(q)
+    left = cnt[:]
+    avail, start, fin, seq = [0.0] * n, [0.0] * n, [0.0] * n, []
+    ready = {k: [] for k in "vatgsn"}
+    free = dict.fromkeys("vatgsn", 0.0)
+    for i in range(n):
+        if left[i] == 0:
+            ready[q[i]].append(i)
+    best, dirty = {}, list("vatgsn")
+    while len(seq) < n:
+        for k in dirty:
+            r = ready[k]
+            if not r:
+                best.pop(k, None)
+                continue
+            f = free[k]
+            t0 = max(f, min([avail[i] for i in r]))
+            bi, bp = -1, -1e18
+            for i in r:
+                if avail[i] <= t0 and base[i] + off[i] > bp:
+                    bp, bi = base[i] + off[i], i
+            best[k] = (t0, bi)
+        k = min(best, key=lambda x: best[x])
+        st, i = best[k]
+        ready[k].remove(i)
+        seq.append(i)
+        start[i], fin[i] = st, st + dur[i]
+        free[k] = st + 60 if k == "s" else (0.0 if k == "n" else fin[i])
+        dirty = [k]
+        for j, soft in nxt[i]:
+            av = free[k] if soft else fin[i] + (40 if q[j] == k else 80)
+            if av > avail[j]:
+                avail[j] = av
+            left[j] -= 1
+            if left[j] == 0:
+                ready[q[j]].append(j)
+                if q[j] not in dirty:
+                    dirty.append(q[j])
+    return max(fin), seq, start, fin
+
+
+TRIES = 4000
+
+
+def improve(ops, gr):
+    rnd = np.random.RandomState(1)
+    n = len(ops)
+    groups = {}
+    for i, o in enumerate(ops):
+        key = (o["q"], tuple(w.rstrip("01234") for w in o["w"]), o["b"] if o["q"] != "t" else tuple(o["r"][:1]), round(o["dur"]))
+        groups.setdefault(key, []).append(i)
+    groups = list(groups.values())
+    off = [0.0] * n
+    best = schedule(gr, off)
+    for _ in range(TRIES):
+        o2 = off[:]
+        for _ in range((1, 1, 2, 3)[int(rnd.randint(4))]):
+            gp = groups[int(rnd.randint(len(groups)))]
+            x = float(rnd.normal()) * (500, 2000, 6000)[int(rnd.randint(3))]
+            if rnd.randint(2):
+                gp = [gp[int(rnd.randint(len(gp)))]]
+            for i in gp:
+                o2[i] += x
+        r = schedule(gr, o2)
+        if r[0] <= best[0]:
+            best, off = r, o2
+    return best
+
+
+PLAN = {}
+
+
+def rank_program(g, core, T, topo):
+    rank = T.rank_of(core)
+    if rank is None:
+        return
+    ops = build(g, T, topo, core)
+    if "seq" not in PLAN:
+        need, order = depend(ops)
+        PLAN["need"] = need
+        PLAN["end"], PLAN["seq"], PLAN["start"], PLAN["fin"] = improve(ops, graph(ops, need, order))
+    need, seq = PLAN["need"], PLAN["seq"]
+    queue = {"v": g.vector, "a": g.scalar, "t": g.tensor, "g": g, "s": g.sync}
+    count, done, known, clock = {}, {}, {}, {}
+    for i in seq:
+        o = ops[i]
+        q = o["q"]
+        kn = known.setdefault(q, {}) if q != "n" else {}
+        for j in sorted(need[i], key=lambda x: -x):
+            s, v = done[j]
+            if q == "t" and ops[j]["q"] == "t" and not o["hard"]:
+                continue
+            if kn.get(s, 0) >= v:
+                continue
+            if q != "n":
+                queue[q].wait_ge(T.sem[s], v)
+            for s2, v2 in clock[j].items():
+                kn[s2] = max(kn.get(s2, 0), v2)
+            kn[s] = max(kn.get(s, 0), v)
+        ins = None
+        for f in o["f"]:
+            ins = f()
+        if o["sem"] is None:
+            s = CNT[q]
+            count[s] = count.get(s, 0) + 1
+            ins.then_inc(T.sem[s], 1)
+        else:
+            s, v = o["sem"]
+            count[s] = count.get(s, 0) + v
+            if q == "s":
+                ins.then_inc(T.sem[s], v)
+        done[i] = (s, count[s])
+        clock[i] = dict(kn)
+    kn = known["g"]
+    for s in count:
+        if kn.get(s, 0) < count[s]:
+            g.wait_ge(T.sem[s], count[s])

@@ -4,6 +4,7 @@ from concourse.mybir import AluOpType as OP, AxisListType, ActivationFunctionTyp
 NST = 5
 XS = 257
 THR = 16384.0
+DIST = ((0, 0), (0, 64), (64, 96), (96, 128))
 BIG = 2.0 ** 20
 ON_DVE = (0, 2, 4, 6)
 
@@ -16,17 +17,17 @@ SCRATCH = {
     "CR": ("sbuf", [128, 384], "bfloat16"), "HI": ("sbuf", [128, 640], "bfloat16"), "TI": ("sbuf", [128, 640], "bfloat16"),
     "X0": ("sbuf", [128, 8 * XS], "bfloat16"), "X1": ("sbuf", [128, 8 * XS], "bfloat16"),
     "AB": ("sbuf", [128, 2048], "bfloat16"), "EQ": ("sbuf", [128, 1024], "bfloat16"),
-    "SEL": ("sbuf", [128, 512], "bfloat16"), "TRI": ("sbuf", [128, 512], "bfloat16"),
+    "SEL": ("sbuf", [128, 512], "bfloat16"), "MK2": ("sbuf", [128, 128], "bfloat16"),
     "cI": ("sbuf", [128, 128], "int32"), "cg": ("sbuf", [128, 640], "int32"), "cm": ("sbuf", [128, 128], "int32"),
     "pc": ("sbuf", [128, 32], "int32"), "pf": ("sbuf", [128, 64], "float32"),
-    "tf": ("sbuf", [128, 128], "float32"), "tf2": ("sbuf", [128, 128], "float32"),
+    "tw": ("sbuf", [128, 128], "float32"), "tf": ("sbuf", [128, 128], "float32"), "tf2": ("sbuf", [128, 128], "float32"),
     "rows": ("sbuf", [128, 1024], "bfloat16"),
     "oXA": ("sbuf", [128, 16], "uint16"),
     "P0": ("psum", [128, 512], "float32"), "P1": ("psum", [128, 512], "float32"), "P2": ("psum", [128, 512], "float32"),
     "P3": ("psum", [128, 512], "float32"), "P4": ("psum", [128, 512], "float32"), "P5": ("psum", [128, 512], "float32"),
     "P6": ("psum", [128, 512], "float32"), "P7": ("psum", [128, 512], "float32"),
 }
-for _n in ("I", "nI", "BO", "cap", "KF", "KC", "ONES", "HALF", "I16", "nI16", "nI256", "D32", "RS", "Kc", "Kn", "CO1", "CO2",
+for _n in ("I", "nI", "BO", "cap", "KF", "KC", "ONES", "HALF", "I16", "nI16", "nI256", "D32", "Kc", "Kn", "CO1", "CO2",
            "WH", "WL", "VH", "VL",
            "zT0", "zT1", "BE", "BD", "DM", "qt", "ivm", "Fs", "Sg", "W", "E1", "wq", "S", "nim"):
     SCRATCH[_n] = ("sbuf", [128, 128], "bfloat16")
@@ -34,7 +35,7 @@ for _n in ("R8", "G16", "hv"):
     SCRATCH[_n] = ("sbuf", [128, 8], "bfloat16")
 for _n in ("Ui", "u", "sq", "s5", "bb", "bbm", "ub", "ubm", "bi", "bm"):
     SCRATCH[_n] = ("sbuf", [128, 128], "int32")
-for _n in ("mb", "sw0", "sw1", "a", "c", "b", "h1", "h2", "h3", "hb1", "hb2", "e2", "s3", "t1", "nb"):
+for _n in ("mb", "sw0", "sw1", "c", "h3", "e2", "s3", "t1", "nb"):
     SCRATCH[_n] = ("sbuf", [128, 128], "float32")
 for _n in ("goff0", "goff1", "soff0", "soff1"):
     SCRATCH[_n] = ("sbuf", [128, 8], "uint16")
@@ -42,13 +43,18 @@ SCRATCH["b16"] = ("sbuf", [128, 128], "uint16")
 for _n in ("vi", "so"):
     SCRATCH[_n] = ("sbuf", [128, 8], "int32")
 SCRATCH["vm"] = ("sbuf", [128, 16], "int32")
-for _n in ("nwi0", "nwi1", "dmin", "hm", "sk", "Ts"):
+for _n in ("nwi0", "nwi1", "dmin", "hm", "sk"):
     SCRATCH[_n] = ("sbuf", [128, 8], "float32")
-for _n in ("MK", "BT0", "BT1", "WE", "A12", "F", "FD", "C", "CD", "L"):
+for _n in ("zr0", "zr1"):
+    SCRATCH[_n] = ("sbuf", [128, 1024], "bfloat16")
+for _n in ("MK", "zr4", "BT0", "BT1", "WE", "A12", "F", "FD", "C", "CD", "L"):
     SCRATCH[_n] = ("sbuf", [128, 256], "bfloat16")
 for _n in ("Ps", "Ns"):
     SCRATCH[_n] = ("sbuf", [128, 384], "bfloat16")
 SCRATCH["B"] = ("sbuf", [128, 128], "bfloat16")
+for _n in ("ab", "h12", "hb12"):
+    SCRATCH[_n] = ("sbuf", [128, 256], "float32")
+SCRATCH["RS"] = ("sbuf", [128, 256], "bfloat16")
 SCRATCH["SM"] = ("sbuf", [128, 128], "bfloat16")
 SCRATCH["XT"] = ("sbuf", [128, 128], "bfloat16")
 
@@ -97,6 +103,9 @@ def build(g, T, topo, core):
         op("t", pe(n), r, grp, *[one(a) for a in calls], banks=(bank,))
         ops[-1]["hard"] = hard
 
+    def pcopy(out, in_, r, w, n=128):
+        op("g", 230 + 2 * n, r, w, lambda: g.affine_select(out, in_, [[1, n]], OP.is_ge, 0.0, 0, 0))
+
     def memset(ap, val, n, w):
         op("v", dv(n, 0.5), (), w, lambda: V.memset(ap, val))
 
@@ -140,11 +149,9 @@ def build(g, T, topo, core):
     memset(T.HALF[:], 0.5, 128, ("HALF",))
     memset(T.rows[:, 0:128], -2080.0, 128, ("rowA",))
     memset(T.rows[:, 128:256], 2336.0, 128, ("rowB",))
-    memset(T.TRI[:], -10.0, 512, ("TRI",))
     memset(T.c[:], 0.0, 128, ("c",))
-    for n in ("h1", "h2", "h3"):
-        memset(T[n][:], 0.0, 128, (n,))
-    op("g", 1000, ("TRI",), ("TRI",), lambda: g.affine_select(T.TRI[:], T.TRI[:], [[0, 4], [-1, 128]], OP.is_ge, 0.0, 0, 1))
+    memset(T.h12[:], 0.0, 512, ("h12",))
+    memset(T.h3[:], 0.0, 256, ("h3",))
     pc, pf = T.pc, T.pf
     pi = pc[:, 0:1]
     copy(pf[:, 0:1], pi, 1, ("pI",), ("f0",))
@@ -167,15 +174,16 @@ def build(g, T, topo, core):
     ts(pc[:, 12:13], pc[:, 10:11], 31, OP.bitwise_and, 1, ("i10",), ("i12",))
     copy(pf[:, 11:12], pc[:, 11:12], 1, ("i11",), ("f11",))
     copy(pf[:, 12:13], pc[:, 12:13], 1, ("i12",), ("f12",))
-    ts(T.VH[:], T.BO[:], pf[:, 11:12], OP.mult, 128, ("BO", "f11"), ("VH",))
-    ts(T.VL[:], T.BO[:], pf[:, 12:13], OP.mult, 128, ("BO", "f12"), ("VL",))
+    act(T.VH[:], T.BO[:], AF.Copy, 128, ("BO", "f11"), ("VH",), scale=pf[:, 11:12])
+    act(T.VL[:], T.BO[:], AF.Copy, 128, ("BO", "f12"), ("VL",), scale=pf[:, 12:13])
     ts(T.MK[:, 0:128], cm, pf[:, 2:3], OP.is_equal, 128, ("cm", "f2"), ("MKa",))
-    copy(T.MK[:, 128:256], T.MK[:, 0:128], 128, ("MKa",), ("MK",), x=0.5)
-    ts(T.RS[:], cm, 0.0, OP.is_gt, 128, ("cm",), ("RS",))
+    act(T.MK[:, 128:256], T.MK[:, 0:128], AF.Copy, 128, ("MKa",), ("MK",))
+    ts(T.RS[:, 0:128], cm, 0.0, OP.is_gt, 128, ("cm",), ("RSa",))
+    act(T.RS[:, 128:256], T.RS[:, 0:128], AF.Copy, 128, ("RSa",), ("RS",))
     ts(T.I[:], cI, pf[:, 0:1], OP.is_equal, 128, ("cI", "f0"), ("I",))
     ts(T.R8[:], T.cI[:, 0:8], pf[:, 1:2], OP.is_equal, 8, ("cI", "f1"), ("R8",))
-    ts(T.tf[:], T.RS[:], 0.5, OP.mult, 128, ("RS",), ("tf",))
-    ts(T.tf2[:], T.RS[:], -512.0, OP.mult, 128, ("RS",), ("tf2",), s2=512.0, o2=OP.add)
+    ts(T.tf[:], T.RS[:, 0:128], 0.5, OP.mult, 128, ("RSa",), ("tf",))
+    ts(T.tf2[:], T.RS[:, 0:128], -512.0, OP.mult, 128, ("RSa",), ("tf2",), s2=512.0, o2=OP.add)
     scan(T.mb[:], T.tf[:], T.tf2[:], OP.mult, OP.add, 128, ("tf", "tf2"), ("mb",))
     tt(T.tf[:], T.mb[:], T.I[:], OP.mult, 128, ("mb", "I"), ("tf",))
     op("v", dv(128), ("tf",), ("f5",), lambda: V.tensor_reduce(pf[:, 5:6], T.tf[:], AxisListType.X, OP.add))
@@ -190,12 +198,11 @@ def build(g, T, topo, core):
     ts(pf[:, 18:20], pf[:, 14:16], -1.0, OP.mult, 2, ("f14", "f15"), ("f18",))
     ts(T.tf[:, 0:8], T.cI[:, 0:8], 16.0, OP.mult, 8, ("cI", "tf"), ("tf",), s2=1024.0, o2=OP.add)
     ts(pf[:, 48:56], T.tf[:, 0:8], pf[:, 2:3], OP.add, 8, ("tf", "f2"), ("iw",))
-    copy(T.BK[:, 0:1024], T.BKI[:], 1024, ("BKI",), ("BK",))
     ts(pc[:, 3:4], pi, 31, OP.bitwise_and, 1, ("pI",), ("i3",))
     copy(pf[:, 3:4], pc[:, 3:4], 1, ("i3",), ("f3",))
     ts(pf[:, 4:5], pf[:, 0:1], 32.0, OP.mult, 1, ("f0",), ("f4",))
     ts(T.SEL[:], T.cg[:, 128:640], pf[:, 3:4], OP.is_equal, 512, ("cg5", "f3"), ("SEL",), s2=-1.0, o2=OP.mult)
-    ts(T.G16[:], T.R8[:], 16.0, OP.mult, 8, ("R8",), ("G16",))
+    act(T.G16[:], T.R8[:], AF.Copy, 8, ("R8",), ("G16",), scale=16.0)
     act(T.KC[:], T.BO[:], AF.Copy, 128, ("BO",), ("KC",), scale=128.0)
     ts(T.rows[:, 512:640], cm, -1.0, OP.mult, 128, ("cm",), ("rowR",), s2=15.0, o2=OP.add)
     ts(T.rows[:, 672:688], T.cI[:, 0:16], 8.0, OP.is_ge, 16, ("cI",), ("rowZ",), s2=-8.0, o2=OP.mult)
@@ -211,17 +218,29 @@ def build(g, T, topo, core):
 
     for name, val in (("KF", THR), ("I16", 16.0), ("nI16", -16.0), ("nI", -1.0), ("nI256", -256.0)):
         scaled(name, val)
-    ts(T.D32[:], T.I[:], pf[:, 4:5], OP.mult, 128, ("I", "f4"), ("D32",), x=0.5)
+    act(T.D32[:], T.I[:], AF.Copy, 128, ("I", "f4"), ("D32",), scale=pf[:, 4:5])
     for t in range(NST):
         scaled("HI", 4096.0 * (8 + t), t)
         if t:
             scaled("TI", float(t), t)
     for j in range(2):
-        memset(T["X%d" % j][:, ::XS], -1.0, 8, ["Xs%d" % j])
+        memset(T["X%d" % j][:, 0:4 * XS:XS], -64.0, 4, ["Xs%d" % j])
+        memset(T["X%d" % j][:, 4 * XS::XS], -1.0, 4, ["Xt%d" % j])
+    tw = T.tw
+    ts(tw[:, 64:72], T.cI[:, 0:8], 0.0, OP.is_equal, 8, ("cI",), ("d1",))
+    for nm_, base_, o in (("n", 1.0 / 64, 0), ("p", 64.0, 24)):
+        memset(tw[:, 72 + o:80 + o], base_, 8, ("d0" + nm_,))
+        scan(tw[:, 80 + o:88 + o], tw[:, 72 + o:80 + o], tw[:, 64:72], OP.mult, OP.add, 8, ("d0" + nm_, "d1"), ("pw" + nm_,))
+        tt(tw[:, 88 + o:96 + o], tw[:, 80 + o:88 + o], T.R8[:], OP.mult, 8, ("pw" + nm_, "R8"), ("px" + nm_,))
+    op("v", dv(8), ("pxn",), ("f57",), lambda: V.tensor_reduce(pf[:, 57:58], tw[:, 88:96], AxisListType.X, OP.add))
+    op("v", dv(8), ("pxp",), ("f58",), lambda: V.tensor_reduce(pf[:, 58:59], tw[:, 112:120], AxisListType.X, OP.add))
+    ts(tw[:, 8:24], T.cm[:, 0:16], pf[:, 2:3], OP.is_gt, 16, ("cm", "f2"), ("wt0",), s2=1.9375, o2=OP.mult)
+    ts(T.rows[:, 900:916], tw[:, 8:24], 0.0625, OP.add, 16, ("wt0", "f57"), ("WT",), s2=pf[:, 57:58], o2=OP.mult)
+    act(T.MK2[:], T.MK[:, 0:128], AF.Copy, 128, ("MKa", "f58"), ("MK2",), scale=pf[:, 58:59])
     ts(pf[:, 20:21], pf[:, 2:3], 1.0, OP.add, 1, ("f2",), ("f20",))
     ts(T.tf2[:], cm, 16.0, OP.mult, 128, ("cm", "f20"), ("tf2",), s2=pf[:, 20:21], o2=OP.add)
     tt(T.Kc[:], T.tf2[:], T.BO[:], OP.mult, 128, ("tf2", "BO"), ("Kc",))
-    ts(T.Kn[:], T.Kc[:], -1.0, OP.mult, 128, ("Kc",), ("Kn",), x=0.5)
+    act(T.Kn[:], T.Kc[:], AF.Copy, 128, ("Kc",), ("Kn",), scale=-1.0)
     ts(pc[:, 4:5], pi, 3, OP.logical_shift_right, 1, ("pI",), ("i4",))
     ts(pc[:, 5:6], pi, 7, OP.bitwise_and, 1, ("pI",), ("i5",))
     copy(pf[:, 21:22], pc[:, 5:6], 1, ("i5",), ("f21",))
@@ -237,7 +256,8 @@ def build(g, T, topo, core):
     memset(T.SM[:, 32:120], 0.0, 88, ("RB",))
     copy(T.SM[:, 72:80], T.R8[:], 8, ("R8",), ("RB",), x=0.5)
     ts(pf[:, 38:44], pf[:, 22:28], 0.5, OP.mult, 6, ["f%d" % j for j in range(22, 28)], ("f38",))
-    ts(pf[:, 29:30], pf[:, 26:27], -4.0, OP.mult, 1, ("f26",), ("f29",))
+    tt(pf[:, 46:47], pf[:, 25:26], pf[:, 26:27], OP.add, 1, ("f25", "f26"), ("f46",))
+    ts(pf[:, 29:30], pf[:, 46:47], -2.0, OP.mult, 1, ("f46",), ("f29",))
     tt(pf[:, 44:45], pf[:, 39:40], pf[:, 38:39], OP.subtract, 1, ("f38",), ("f44",))
     tt(pf[:, 28:29], pf[:, 44:45], pf[:, 29:30], OP.add, 1, ("f44", "f29"), ("f28",))
     tt(pf[:, 45:46], pf[:, 39:40], pf[:, 40:41], OP.add, 1, ("f38",), ("f45",))
@@ -256,6 +276,10 @@ def build(g, T, topo, core):
 
     def prep(t):
         z, k, d = zap(t), zk(t), t % 2
+        for j in range(4):
+            pcopy(T.zr4[:, j::4], z[:, 0:64], (k,), ("zr4%d" % j,), 64)
+        for j in range(4):
+            pcopy(T["zr%d" % d][:, j::4], T.zr4[:], ["zr4%d" % i for i in range(4)], ("zr%d" % d,) if j == 3 else ("zq%d%d" % (d, j),), 256)
         mm(256, (k, "WH", "WL"), "P6", (P6[:, 0:128], T.WH[:], z, True, False), (P6[:, 0:128], T.WL[:], z, False, True))
         mm(256, (k, "VH", "VL"), "P6", (P6[:, 128:256], T.VH[:], z, True, False), (P6[:, 128:256], T.VL[:], z, False, True))
         copy(T.Ui[:], P6[:, 0:128], 128, (), ("Ui",), banks=("P6",))
@@ -265,7 +289,7 @@ def build(g, T, topo, core):
         tt(P6[:, 256:384], T.s5[:], P6[:, 128:256], OP.add, 128, ("s5",), ("base",), banks=("P6",), x=1.0)
         sw = T["sw%d" % d]
         tt(T.mb[:], P6[:, 256:384], T.MK[:, 0:128], OP.mult, 128, ("base", "MKa"), ("mb",), banks=("P6",), x=1.0)
-        scan(sw[:], T.RS[:], T.mb[:], OP.mult, OP.add, 128, ("RS", "mb"), ("sw%d" % d,))
+        scan(sw[:], T.RS[:, 0:128], T.mb[:], OP.mult, OP.add, 128, ("RSa", "mb"), ("sw%d" % d,))
         mm(128, (k, "I"), "P6", (P6[:, 384:512], z, T.I[:], True, True))
         act(T["zT%d" % d][:], P6[:, 384:512], AF.Copy, 128, (), ("zT%d" % d,), banks=("P6",))
 
@@ -277,23 +301,23 @@ def build(g, T, topo, core):
             ts(T.ubm[:], T.ub[:], 128, OP.bitwise_and, 128, ("ub",), ("ubm",))
             bt = T["BT%d" % d]
             ts(bt[:, 0:128], T.ubm[:], -1.0 / 128, OP.mult, 128, ("ubm",), ("bta%d" % d,))
-            copy(bt[:, 128:256], bt[:, 0:128], 128, ("bta%d" % d,), ("BT%d" % d,), x=0.5)
+            pcopy(bt[:, 128:256], bt[:, 0:128], ("bta%d" % d,), ("BT%d" % d,))
         ts(T.bbm[:], T.bb[:], 512, OP.bitwise_and, 128, ("bb",), ("bbm",))
         ts(T.BD[:], T.bbm[:], pf[:, 16:17], OP.mult, 128, ("bbm", "f16", "f18"), ("BD",), s2=pf[:, 18:19], o2=OP.add)
         ts(T.BE[:], T.bbm[:], pf[:, 17:18], OP.mult, 128, ("bbm", "f16", "f18"), ("BE",), s2=pf[:, 19:20], o2=OP.add)
         for h in range(2):
             for j in range(2):
-                calls = [] if j else [(P0[:, 0:512], T.I[:], T.TRI[:], True, False)]
+                calls = []
                 for i in range(2):
                     bx = (T.BD if i else T.BE)[64 * h + 32 * j:64 * h + 32 * j + 32, :]
-                    calls.append((P0[:, 256 * j + 128 * i:256 * j + 128 * i + 128], bx, bx, False, j + i == 2))
-                mm(256 if j else 768, ("I", "TRI", "BD", "BE"), "P0", *calls, grp=("gdup",), hard=bool(j))
+                    calls.append((P0[:, 256 * j + 128 * i:256 * j + 128 * i + 128], bx, bx, True, True))
+                mm(256, ("BD", "BE"), "P0", *calls, grp=("gdup",), hard=bool(j))
             act(T.EQ[:, 512 * h:512 * h + 512], P0[:], AF.Relu, 512, (), ("EQ%d" % h,), bias=-9.0, banks=("P0",))
-        mm(512, ("EQ0", "EQ1", "ONES"), "P6",
-           *[(P6[:, 16 * j:16 * j + 16], T.EQ[:, 128 * j:128 * j + 128], T.ONES[:, 0:16], True, True) for j in range(8)])
-        tt(T.DM[:], P6[:, 0:128], T.MK[:, 0:128], OP.mult, 128, ("MKa",), ("DM",), banks=("P6",), x=1.0)
-        mm(64, ("DM", "R8"), "P6", (P6[:, 128:136], T.DM[:], T.R8[:], True, True))
-        ts(T.dmin[:], P6[:, 128:136], 1.0, OP.min, 8, (), ("dmin",), banks=("P6",))
+        mm(512, ("EQ0", "EQ1", "WT"), "P0",
+           *[(P0[:, 16 * j:16 * j + 16], T.EQ[:, 128 * j:128 * j + 128], T.rows[:, 900:916], True, True) for j in range(8)])
+        tt(T.DM[:], P0[:, 0:128], T.MK2[:], OP.mult, 128, ("MK2",), ("DM",), banks=("P0",), x=1.0)
+        mm(64, ("DM", "R8"), "P0", (P0[:, 128:136], T.DM[:], T.R8[:], True, True))
+        act(T.dmin[:], P0[:, 128:136], AF.Sign, 8, (), ("dmin",), bias=-1.75, banks=("P0",))
         tt(T["nwi%d" % d][:], T.dmin[:], pf[:, 48:56], OP.mult, 8, ("dmin", "iw"), ("nwi%d" % d,))
 
     def voff(t):
@@ -317,28 +341,49 @@ def build(g, T, topo, core):
         go, gk = T["goff%d" % d][:, 0:8], "goff%d" % d
         X, xk = T["X%d" % d], "X%d" % d
         win = T.BK[:, 0:1024]
-        copy(T.bi[:], win.indirect(go), 128, ("BK", gk), ("bi",), x=1.6)
-        act(T.qt[:], win.indirect(go), AF.Identity, 128, ("BK", gk), ("qt",), bias=129.5 + 2.0 ** -14, scale=1.0 / 4096, x=1.6)
+        qb = {"bias": 129.5 + 2.0 ** -14, "scale": 1.0 / 4096}
+        if t == 0:
+            copy(T.bi[:], T.BKI[:].indirect(go), 128, ("BKI", gk), ("bi",), x=1.6)
+            copy(T.nb[:], T.bi[:], 128, ("bi",), ("nb",))
+            act(T.qt[:], T.nb[:], AF.Identity, 128, ("nb",), ("qt",), **qb)
+            copy(T.BK[:, 0:1024], T.BKI[:], 1024, ("BKI",), ("BK",))
+        else:
+            copy(T.bi[:], win.indirect(go), 128, ("BK", gk), ("bi",), x=1.6)
+            act(T.qt[:], win.indirect(go), AF.Identity, 128, ("BK", gk), ("qt",), x=1.6, **qb)
         ts(T.bm[:], T.bi[:], 4095, OP.bitwise_and, 128, ("bi",), ("bm",))
         copy(T.b16[:], T.bm[:], 128, ("bm",), ("b16",))
         act(T.Fs[:], T.qt[:], AF.Sign, 128, ("qt",), ("Fs",), bias=-(131.5 + t))
         for c in range(8):
             off = T.b16[:, 16 * c:16 * c + 16]
             out = X[:, XS * c + 1:XS * c + 257]
-            if c in ON_DVE:
-                copy(out, T.G[:].indirect(off), 256, ("G", "b16"), (xk + str(c),), x=1.6)
+            if c < 4:
+                tt(out, T.G[:].indirect(off), T["zr%d" % d][:, 256 * c:256 * c + 256], OP.subtract, 256,
+                   ("G", "b16", "zr%d" % d) + tuple("zq%d%d" % (d, j) for j in range(3)), (xk + str(c),), x=1.6)
             else:
                 act(out, T.G[:].indirect(off), AF.Copy, 256, ("G", "b16"), (xk + str(c),), x=1.6)
-        act(T.ivm[:], T.IM[:, 0:1024].indirect(go), AF.Identity, 128, ("IM", gk), ("ivm",), bias=-1.0, x=1.6)
-        mm(256, (k, "ivm", "I", "nI"), "P7", (P7[:, 0:128], T.I[:], z, True, False), (P7[:, 0:128], T.nI[:], T.ivm[:], False, True))
-        act(T.Sg[:], P7[:, 0:128], AF.Sign, 128, (), ("Sg",), bias=-1.5, banks=("P7",))
         mm(256, ("qt", "I16", "ONES", "rowA"), "P7", (P7[:, 128:256], one1, T.rows[0:1, 0:128], True, False),
            (P7[:, 128:256], T.qt[:], T.I16[:], False, True))
         mm(384, ("qt", "nI16", "ONES", "rowB", "rowR"), "P7", (P7[:, 256:384], one1, T.rows[0:1, 128:256], True, False),
            (P7[:, 256:384], one1, T.rows[0:1, 512:640], False, False), (P7[:, 256:384], T.qt[:], T.nI16[:], False, True))
+        if True:
+            mm(64, ("Fs", "R8"), "P7", (P7[:, 384:392], T.Fs[:], T.R8[:], True, True))
+        act(T.ivm[:], T.IM[:, 0:1024].indirect(go), AF.Identity, 128, ("IM", gk), ("ivm",), bias=-1.0, x=1.6)
+        mm(256, (k, "ivm", "I", "nI"), "P7", (P7[:, 0:128], T.I[:], z, True, False), (P7[:, 0:128], T.nI[:], T.ivm[:], False, True))
+        act(T.Sg[:], P7[:, 0:128], AF.Sign, 128, (), ("Sg",), bias=-1.5, banks=("P7",))
         mm(256, ("Fs", "KF", "rowR", "ONES"), "P5", (P5[:, 0:128], one1, T.rows[0:1, 512:640], True, False),
            (P5[:, 0:128], T.Fs[:], T.KF[:], False, False), grp=("gkey",))
+        def dist(e):
+            lo, hi = DIST[e]
+            if hi > lo:
+                mm(16 * max(hi - lo, 8), ["AB%d%d" % (i, j) for i in range(lo // 32, hi // 32) for j in range(2)] + ["G16"], "P5",
+                   *[(P5[lo:hi, kk:128:16], T.AB[:, 16 * lo + kk:16 * hi:16], T.G16[:], False, kk == 15) for kk in range(16)],
+                   grp=("gkey",))
         for e in range(4):
+            if e < 2:
+                for c in (2 * e, 2 * e + 1):
+                    act(T.AB[:, 256 * c:256 * c + 256], X[:, XS * c + 1:XS * c + 257], AF.Abs, 256, (xk + str(c),), ("AB%d%d" % (e, c % 2),))
+                dist(e)
+                continue
             bank = "P%d" % (1 + e % 2)
             pb = T[bank]
             zt = T["zT%d" % d][32 * e:32 * e + 32, :]
@@ -346,48 +391,39 @@ def build(g, T, topo, core):
             for j in range(2):
                 c = 2 * e + j
                 mm(256, (xk + str(c), "I"), bank, (pb[:, 256 * j:256 * j + 256], T.I[:], X[:, XS * c + 1:XS * c + 257], False, j == 1), grp=("g" + bank,))
-            act(T.AB[:, 512 * e:512 * e + 512], pb[:], AF.Abs, 512, (), ("AB%d" % e,), banks=(bank,))
-            if e == 2:
-                mm(1024, ("AB0", "AB1", "AB2", "G16"), "P5",
-                   *[(P5[0:96, kk:128:16], T.AB[:, kk:1536:16], T.G16[:], False, kk == 15) for kk in range(16)], grp=("gkey",))
-            if e == 3:
-                mm(512, ("AB3", "G16"), "P5",
-                   *[(P5[96:128, kk:128:16], T.AB[:, 1536 + kk:2048:16], T.G16[:], False, kk == 15) for kk in range(16)], grp=("gkey",))
+            act(T.AB[:, 512 * e:512 * e + 512], pb[:], AF.Abs, 512, (), ("AB%d0" % e, "AB%d1" % e), banks=(bank,))
+            dist(e)
         dups(t)
         soff(t)
-        copy(T.G[:, t::32], z, 128, (k,), ("G",), x=0.5)
+        pcopy(T.G[:, t::32], z, (k,), ("G",))
         mm(192, ("Sg", "KC", "R8"), "P7", (P7[:, 0:128], T.Sg[:], T.KC[:], True, True), (P7[:, 392:400], T.Sg[:], T.R8[:], True, True))
         act(T.cap[:], P7[:, 0:128], AF.Relu, 128, (), ("cap",), banks=("P7",))
         ts(T.sk[:], P7[:, 392:400], 1.0, OP.is_ge, 8, (), ("sk",), banks=("P7",))
         tt(P7[:, 128:256], P7[:, 128:256], T.cap[:], OP.min, 128, ("cap",), ("q16s",), banks=("P7",), x=1.0)
-        ts(T.Ts[:], T.sk[:], -BIG, OP.mult, 8, ("sk",), ("Ts",), s2=BIG + THR, o2=OP.add)
+        ts(T.hm[:], P7[:, 384:392], -12.0, OP.min, 8, (), ("hm",), s2=16.0, o2=OP.add, banks=("P7",))
+        tt(T.hv[:], T.hm[:], T.sk[:], OP.mult, 8, ("hm", "sk"), ("hv",))
         if last:
             load(T.ygeno[:], T.G[:], ("yg",), 7000, r=("G",))
         else:
-            mm(64, ("Fs", "R8"), "P7", (P7[:, 384:392], T.Fs[:], T.R8[:], True, True))
-            ts(T.hm[:], P7[:, 384:392], -12.0, OP.min, 8, (), ("hm",), s2=16.0, o2=OP.add, banks=("P7",))
-            tt(T.hv[:], T.hm[:], T.sk[:], OP.mult, 8, ("hm", "sk"), ("hv",))
             mm(64, ("hv", "HALF"), "P7", (P7[:, 400:408], T.HALF[:], T.hv[:], True, True))
             op("v", dv(8), (), ("A",), lambda: V.tensor_reduce(pf[:, 63:64], P7[:, 400:408], AxisListType.X, OP.add), banks=("P7",))
             prep(t + 1)
             voff(t + 1)
         key = P5[:, 0:128]
-        scan(T.a[:], T.RS[:], key, OP.mult, OP.max, 128, ("RS",), ("a",), banks=("P5",))
-        tt(T.c[:, 1:128], T.a[:, 0:127], P5[:, 1:128], OP.min, 128, ("a",), ("c",), banks=("P5",), x=1.0)
-        scan(T.b[:], T.c[:], T.RS[:], OP.max, OP.mult, 128, ("c", "RS"), ("b",))
-        ts(T.h2[:, 0::16], T.b[:, 15::16], THR, OP.max, 8, ("b",), ("h2",))
-        scan(T.hb2[:], T.RS[:], T.h2[:], OP.mult, OP.add, 128, ("h2", "RS"), ("hb2",))
-        tt(T.W[:], key, T.hb2[:], OP.is_ge, 128, ("hb2",), ("W",), banks=("P5",), x=1.0)
+        RS = T.RS[:, 0:128]
+        scan(T.ab[:, 0:128], RS, key, OP.mult, OP.max, 128, ("RSa",), ("a",), banks=("P5",))
+        tt(T.c[:, 1:128], T.ab[:, 0:127], P5[:, 1:128], OP.min, 128, ("a",), ("c",), banks=("P5",), x=1.0)
+        scan(T.ab[:, 128:256], T.c[:], RS, OP.max, OP.mult, 128, ("c", "RSa"), ("b",))
+        ts(T.h12[:, 0::16], T.ab[:, 15::16], THR, OP.max, 16, ("a", "b"), ("h12",))
+        scan(T.hb12[:], T.RS[:], T.h12[:], OP.mult, OP.add, 256, ("h12", "RS"), ("hb12",))
+        tt(T.W[:], key, T.hb12[:, 128:256], OP.is_ge, 128, ("hb12",), ("W",), banks=("P5",), x=1.0)
+        tt(T.E1[:], key, T.hb12[:, 0:128], OP.is_ge, 128, ("hb12",), ("E1",), banks=("P5",), x=1.0)
         tt(T.wq[:], P7[:, 128:256], T.W[:], OP.mult, 128, ("W", "q16s"), ("wq",), banks=("P7",), x=1.0)
         tt(T.e2[:], P7[:, 256:384], T.wq[:], OP.add, 128, ("wq",), ("e2",), banks=("P7",), x=1.0)
-        scan(T.s3[:], T.RS[:], T.e2[:], OP.mult, OP.max, 128, ("e2", "RS"), ("s3",))
+        scan(T.s3[:], RS, T.e2[:], OP.mult, OP.max, 128, ("e2", "RSa"), ("s3",))
         copy(T.h3[:, 0::16], T.s3[:, 15::16], 8, ("s3",), ("h3",))
-        scan(P5[:, 384:512], T.RS[:], T.h3[:], OP.mult, OP.add, 128, ("h3", "RS"), ("hb3",), banks=("P5",))
+        scan(P5[:, 384:512], RS, T.h3[:], OP.mult, OP.add, 128, ("h3", "RSa"), ("hb3",), banks=("P5",))
         tt(T.S[:], T.e2[:], P5[:, 384:512], OP.is_equal, 128, ("e2", "hb3"), ("S",), banks=("P5",), x=1.0)
-        ts(T.h1[:, 0::16], T.a[:, 15::16], THR, OP.max, 8, ("a",), ("h1",))
-        scan(T.hb1[:], T.RS[:], T.h1[:], OP.mult, OP.add, 128, ("h1", "RS"), ("hb1",))
-        tt(T.E1[:], key, T.hb1[:], OP.is_ge, 128, ("hb1",), ("E1",), banks=("P5",), x=1.0)
-        tt(T.SM[:, 120:128], T.a[:, 15::16], T.Ts[:], OP.is_ge, 8, ("a", "Ts"), ("XBh",))
         mm(128, ("wq", "nI256"), "P7", (P7[:, 0:128], T.wq[:], T.nI256[:], True, True))
         calls = [(P5[:, 256:384], T.S[:], T.D32[:], True, False)]
         if t:
@@ -409,10 +445,9 @@ def build(g, T, topo, core):
            (P3[:, 0:16], one1, T.rows[0:1, 656:672], False, False),
            (P3[:, 0:8], T.L[:, 0:128], T.R8[:], False, False), (P3[:, 8:16], T.L[:, 128:256], T.R8[:], False, True))
         copy(T.oXA[:], P3[:, 0:16], 16, (), ("oXA",), banks=("P3",))
-        act(T.A12[:], X[:].indirect(T.oXA[:, 0:16]), AF.Copy, 256, ["oXA", "Xs%d" % d] + [xk + str(c) for c in range(8)], ("A12",), x=1.6)
-        for j in range(2):
-            mm(256, ("A12", k, "I", "nI"), "P4", (P4[:, 128 * j:128 * j + 128], T.nI[:], z, True, False),
-               (P4[:, 128 * j:128 * j + 128], T.I[:], T.A12[:, 128 * j:128 * j + 128], False, True))
+        act(T.A12[:], X[:].indirect(T.oXA[:, 0:16]), AF.Copy, 256, ["oXA", "Xs%d" % d, "Xt%d" % d] + [xk + str(c) for c in range(8)], ("A12",), x=1.6)
+        mm(384, ("A12", k, "I", "nI"), "P4", (P4[:, 0:256], T.I[:], T.A12[:], True, False),
+           (P4[:, 64:128], T.nI[:], z[:, 64:128], False, False), (P4[:, 192:256], T.nI[:], z[:, 64:128], False, True))
         mm(256, ("A12", "I", "nI"), "P4", (P4[:, 256:384], T.I[:], T.A12[:, 128:256], True, False),
            (P4[:, 256:384], T.nI[:], T.A12[:, 0:128], False, True))
         act(T.Ps[:], P4[:, 0:384], AF.Sign, 384, (), ("Ps",), bias=-0.5, banks=("P4",))
@@ -423,8 +458,8 @@ def build(g, T, topo, core):
         mm(384, ("Ps", "RB"), "P4", cnt(0, T.Ps, 0, True), cnt(3, T.Ps, 1), cnt(4, T.Ps, 2), grp=("gcnt",))
         mm(384, ("Ns", "RB"), "P4", cnt(1, T.Ns, 0), cnt(2, T.Ns, 1), cnt(5, T.Ns, 2, False, True), grp=("gcnt",))
         act(T.B[0:48, :], P4[0:48, 384:512], AF.Sign, 128, (), ("B",), bias=-1.0, banks=("P4",))
-        mm(192, ("B", "M10", "M11", "M12", "M13", "XBh", "I"), "P3", (P3[0:32, 0:128], T.SM[0:48, 0:32], T.B[0:48, :], True, True),
-           (P3[32:40, 0:128], T.SM[:, 120:128], T.I[:], True, True))
+        mm(192, ("B", "M10", "M11", "M12", "M13", "hv", "I"), "P3", (P3[0:32, 0:128], T.SM[0:48, 0:32], T.B[0:48, :], True, True),
+           (P3[32:40, 0:128], T.hv[:], T.I[:], True, True))
         act(T.XT[0:40, :], P3[0:40, 0:128], AF.Sign, 128, (), ("XT",), bias=-1.0, banks=("P3",))
         mm(256, ("XT", "CO1", "CO2"), "P0", (P0[:, 0:128], T.CO1[0:40, :], T.XT[0:40, :], True, True),
            (P0[:, 128:256], T.CO2[0:40, :], T.XT[0:40, :], True, True))
@@ -477,7 +512,7 @@ def depend(ops):
                 h[0], h[1], h[2] = o["q"], h[2], set()
             need |= h[1]
             h[2].add(i)
-        if o["q"] in ("s", "g"):
+        if o["q"] == "s":
             if o["q"] in lastq:
                 order.add(lastq[o["q"]])
             lastq[o["q"]] = i
@@ -488,22 +523,7 @@ def depend(ops):
     return rdy, prev
 
 
-def graph(ops, need, order):
-    n = len(ops)
-    nxt = [[] for _ in range(n)]
-    cnt = [0] * n
-    for i in range(n):
-        for j in sorted(need[i] | order[i]):
-            nxt[j].append((i, j not in need[i]))
-            cnt[i] += 1
-    base = [0.0] * n
-    for i in range(n - 1, -1, -1):
-        base[i] = ops[i]["dur"] + max([base[j] + 40 for j, _ in nxt[i]], default=0.0)
-    return [o["q"] for o in ops], [o["dur"] for o in ops], nxt, cnt, base
-
-
-def schedule(gr, off):
-    q, dur, nxt, cnt, base = gr
+def schedule(q, dur, nxt, cnt, key):
     n = len(q)
     left = cnt[:]
     avail, start, fin, seq = [0.0] * n, [0.0] * n, [0.0] * n, []
@@ -523,8 +543,8 @@ def schedule(gr, off):
             t0 = max(f, min([avail[i] for i in r]))
             bi, bp = -1, -1e18
             for i in r:
-                if avail[i] <= t0 and base[i] + off[i] > bp:
-                    bp, bi = base[i] + off[i], i
+                if avail[i] <= t0 and key[i] > bp:
+                    bp, bi = key[i], i
             best[k] = (t0, bi)
         k = min(best, key=lambda x: best[x])
         st, i = best[k]
@@ -533,8 +553,8 @@ def schedule(gr, off):
         start[i], fin[i] = st, st + dur[i]
         free[k] = st + 60 if k == "s" else (0.0 if k == "n" else fin[i])
         dirty = [k]
-        for j, soft in nxt[i]:
-            av = free[k] if soft else fin[i] + (40 if q[j] == k else 80)
+        for j, lag in nxt[i]:
+            av = fin[i] + lag
             if av > avail[j]:
                 avail[j] = av
             left[j] -= 1
@@ -545,31 +565,36 @@ def schedule(gr, off):
     return max(fin), seq, start, fin
 
 
-TRIES = 4000
+TRIES = 1500
 
 
-def improve(ops, gr):
-    rnd = np.random.RandomState(1)
+def improve(ops, need, order):
+    rnd = np.random.RandomState(3)
     n = len(ops)
-    groups = {}
-    for i, o in enumerate(ops):
-        key = (o["q"], tuple(w.rstrip("01234") for w in o["w"]), o["b"] if o["q"] != "t" else tuple(o["r"][:1]), round(o["dur"]))
-        groups.setdefault(key, []).append(i)
-    groups = list(groups.values())
-    off = [0.0] * n
-    best = schedule(gr, off)
+    q, dur = [o["q"] for o in ops], [o["dur"] for o in ops]
+    nxt, prv = [[] for _ in range(n)], [[] for _ in range(n)]
+    for i in range(n):
+        for j in sorted(need[i] | order[i]):
+            lag = (40 if q[i] == q[j] else 80) if j in need[i] else 60 - dur[j]
+            nxt[j].append((i, lag))
+            prv[i].append((j, lag))
+    cur = [0.0] * n
+    for i in range(n - 1, -1, -1):
+        cur[i] = dur[i] + max([cur[j] + 40 for j, _ in nxt[i]], default=0.0)
+    best = None
     for _ in range(TRIES):
-        o2 = off[:]
-        for _ in range((1, 1, 2, 3)[int(rnd.randint(4))]):
-            gp = groups[int(rnd.randint(len(groups)))]
-            x = float(rnd.normal()) * (500, 2000, 6000)[int(rnd.randint(3))]
-            if rnd.randint(2):
-                gp = [gp[int(rnd.randint(len(gp)))]]
-            for i in gp:
-                o2[i] += x
-        r = schedule(gr, o2)
-        if r[0] <= best[0]:
-            best, off = r, o2
+        r = schedule(q, dur, nxt, [len(x) for x in prv], cur)
+        for _ in range(4):
+            key = schedule(q, dur, prv, [len(x) for x in nxt], r[3])[3]
+            r2 = schedule(q, dur, nxt, [len(x) for x in prv], key)
+            if best is None or min(r, r2)[0] < best[0]:
+                best = r2 if r2[0] < r[0] else r
+            if r2[0] >= r[0] - 1:
+                break
+            r = r2
+        key = schedule(q, dur, prv, [len(x) for x in nxt], best[3])[3]
+        sg = (100.0, 400.0, 1500.0)[int(rnd.randint(3))]
+        cur = [key[i] + sg * float(x) for i, x in enumerate(rnd.normal(size=n))]
     return best
 
 
@@ -584,7 +609,7 @@ def rank_program(g, core, T, topo):
     if "seq" not in PLAN:
         need, order = depend(ops)
         PLAN["need"] = need
-        PLAN["end"], PLAN["seq"], PLAN["start"], PLAN["fin"] = improve(ops, graph(ops, need, order))
+        PLAN["end"], PLAN["seq"], PLAN["start"], PLAN["fin"] = improve(ops, need, order)
     need, seq = PLAN["need"], PLAN["seq"]
     queue = {"v": g.vector, "a": g.scalar, "t": g.tensor, "g": g, "s": g.sync}
     count, done, known, clock = {}, {}, {}, {}
@@ -616,7 +641,7 @@ def rank_program(g, core, T, topo):
             if q == "s":
                 ins.then_inc(T.sem[s], v)
         done[i] = (s, count[s])
-        clock[i] = dict(kn)
+        clock[i] = {} if q == "n" else dict(kn)
     kn = known["g"]
     for s in count:
         if kn.get(s, 0) < count[s]:

import numpy as np
from concourse.mybir import AluOpType as OP, AxisListType, ActivationFunctionType as AF

NST = 5
XS = 257
THR = 16384.0
DIST = ((0, 0), (0, 64), (64, 96), (96, 128))
BIG = 2.0 ** 20
ON_DVE = (0, 2, 4, 6)

SCRATCH = {
    "G": ("sbuf", [128, 4096], "bfloat16"), "BKI": ("sbuf", [128, 1024], "int32"),
    "BK": ("sbuf", [128, 1152], "float32"), "IM": ("sbuf", [128, 1152], "bfloat16"),
    "ZB": ("sbuf", [128, 256], "bfloat16"), "WI": ("sbuf", [128, 1], "int32"),
    "Z1": ("sbuf", [128, 128], "bfloat16"), "Z2": ("sbuf", [128, 128], "bfloat16"),
    "Z3": ("sbuf", [128, 128], "bfloat16"), "Z4": ("sbuf", [128, 128], "bfloat16"),
    "CR": ("sbuf", [128, 384], "bfloat16"), "HI": ("sbuf", [128, 640], "bfloat16"), "TI": ("sbuf", [128, 640], "bfloat16"),
    "X0": ("sbuf", [128, 8 * XS], "bfloat16"), "X1": ("sbuf", [128, 8 * XS], "bfloat16"),
    "AB": ("sbuf", [128, 2048], "bfloat16"), "EQ": ("sbuf", [128, 1024], "bfloat16"),
    "SEL": ("sbuf", [128, 512], "bfloat16"), "MK2": ("sbuf", [128, 128], "bfloat16"),
    "cI": ("sbuf", [128, 128], "int32"), "cg": ("sbuf", [128, 640], "int32"), "cm": ("sbuf", [128, 128], "int32"),
    "pc": ("sbuf", [128, 32], "int32"), "pf": ("sbuf", [128, 64], "float32"),
    "tw": ("sbuf", [128, 128], "float32"), "tf": ("sbuf", [128, 128], "float32"), "tf2": ("sbuf", [128, 128], "float32"),
    "rows": ("sbuf", [128, 1024], "bfloat16"),
    "oXA": ("sbuf", [128, 16], "uint16"),
    "P0": ("psum", [128, 512], "float32"), "P1": ("psum", [128, 512], "float32"), "P2": ("psum", [128, 512], "float32"),
    "P3": ("psum", [128, 512], "float32"), "P4": ("psum", [128, 512], "float32"), "P5": ("psum", [128, 512], "float32"),
    "P6": ("psum", [128, 512], "float32"), "P7": ("psum", [128, 512], "float32"),
}
for _n in ("I", "nI", "BO", "cap", "KF", "KC", "ONES", "HALF", "I16", "nI16", "nI256", "D32", "Kc", "Kn", "CO1", "CO2",
           "WH", "WL", "VH", "VL",
           "zT0", "zT1", "BE", "BD", "DM", "qt", "ivm", "Fs", "Sg", "W", "E1", "wq", "S", "nim"):
    SCRATCH[_n] = ("sbuf", [128, 128], "bfloat16")
for _n in ("R8", "G16", "hv"):
    SCRATCH[_n] = ("sbuf", [128, 8], "bfloat16")
for _n in ("Ui", "u", "sq", "s5", "bb", "bbm", "ub", "ubm", "bi", "bm"):
    SCRATCH[_n] = ("sbuf", [128, 128], "int32")
for _n in ("mb", "sw0", "sw1", "c", "h3", "e2", "s3", "t1", "nb"):
    SCRATCH[_n] = ("sbuf", [128, 128], "float32")
for _n in ("goff0", "goff1", "soff0", "soff1"):
    SCRATCH[_n] = ("sbuf", [128, 8], "uint16")
SCRATCH["b16"] = ("sbuf", [128, 128], "uint16")
for _n in ("vi", "so"):
    SCRATCH[_n] = ("sbuf", [128, 8], "int32")
SCRATCH["vm"] = ("sbuf", [128, 16], "int32")
for _n in ("nwi0", "nwi1", "dmin", "hm", "sk"):
    SCRATCH[_n] = ("sbuf", [128, 8], "float32")
for _n in ("zr0", "zr1"):
    SCRATCH[_n] = ("sbuf", [128, 1024], "bfloat16")
for _n in ("MK", "zr4", "BT0", "BT1", "WE", "A12", "F", "FD", "C", "CD", "L"):
    SCRATCH[_n] = ("sbuf", [128, 256], "bfloat16")
for _n in ("Ps", "Ns"):
    SCRATCH[_n] = ("sbuf", [128, 384], "bfloat16")
SCRATCH["B"] = ("sbuf", [128, 128], "bfloat16")
for _n in ("ab", "h12", "hb12"):
    SCRATCH[_n] = ("sbuf", [128, 256], "float32")
SCRATCH["RS"] = ("sbuf", [128, 256], "bfloat16")
SCRATCH["SM"] = ("sbuf", [128, 128], "bfloat16")
SCRATCH["XT"] = ("sbuf", [128, 128], "bfloat16")

SEMAPHORES = ["sv", "sa", "st", "sg", "ls"] + ["dm%d" % i for i in range(8)] + ["rz%d" % t for t in range(1, 5)]
CNT = {"v": "sv", "a": "sa", "t": "st", "g": "sg"}


def build(g, T, topo, core):
    ops = []

    def op(q, dur, reads, writes, *fns, banks=(), sem=None):
        ops.append({"q": q, "dur": dur, "r": tuple(reads), "w": tuple(writes), "f": fns, "b": tuple(banks), "sem": sem})

    V, S, PE = g.vector, g.scalar, g.tensor

    def dv(n, x=1.0):
        return 35 + max(64.0, n * x) * 0.83 * 1.2

    def ac(n):
        return 60 + max(64.0, n) * 0.83 * 1.2

    def pe(n):
        return 60 + n * 0.6

    def copy(out, in_, n, r, w, banks=(), x=1.0):
        op("v", dv(n, x), r, w, lambda: V.tensor_copy(out, in_), banks=banks)

    def tt(out, in0, in1, o, n, r, w, banks=(), x=2.0):
        op("v", dv(n, x), r, w, lambda: V.tensor_tensor(out, in0, in1, o), banks=banks)

    def ts(out, in0, s1, o1, n, r, w, s2=None, o2=None, banks=(), x=1.0):
        if o2 is None:
            op("v", dv(n, x), r, w, lambda: V.tensor_scalar(out, in0, s1, None, o1), banks=banks)
        else:
            op("v", dv(n, x), r, w, lambda: V.tensor_scalar(out, in0, s1, s2, o1, o2), banks=banks)

    def scan(out, d0, d1, o0, o1, n, r, w, banks=()):
        op("v", dv(n), r, w, lambda: V.tensor_tensor_scan(out, d0, d1, 0.0, o0, o1), banks=banks)

    def act(out, in_, f, n, r, w, bias=0.0, scale=1.0, banks=(), x=1.0):
        op("a", ac(n * x), r, w, lambda: S.activation(out, in_, f, bias, scale), banks=banks)

    def mm(n, r, bank, *calls, grp=(), hard=False):
        def one(a):
            return lambda: PE.matmul(*a)
        op("t", pe(n), r, grp, *[one(a) for a in calls], banks=(bank,))
        ops[-1]["hard"] = hard

    def pcopy(out, in_, r, w, n=128):
        op("g", 230 + 2 * n, r, w, lambda: g.affine_select(out, in_, [[1, n]], OP.is_ge, 0.0, 0, 0))

    def memset(ap, val, n, w):
        op("v", dv(n, 0.5), (), w, lambda: V.memset(ap, val))

    nd = [0]

    def load(out, in_, w, dur, r=()):
        s = "dm%d" % nd[0]
        nd[0] += 1
        op("s", dur, r, w, lambda: g.sync.dma_start(out, in_), sem=(s, 16))

    load(T.WI[:], T.wt[:], ("WI",), 2000)
    load(T.ZB[:], T.bites[:], ("ZB",), 2200)
    load(T.BKI[:], T.bank[:], ("BKI",), 4000)
    load(T.IM[:, 0:1024], T.immun[:], ("IM",), 5000)
    load(T.G[:], T.geno[:], ("G",), 8500)

    rank = T.rank_of(core)
    cores = list(T.cores)
    nr = len(cores)

    def engs(src, dst):
        return topo.engines(src, dst)[:8]

    def send(src_ap, key, dst, t):
        e = engs(core, dst)
        m = 0
        for x in e:
            m |= 1 << x
        a = topo.addr(dst)
        zt = T["Z%d" % t]
        op("g", 300, (key,), ("sent%d" % t,), lambda: g.remote_dma(zt[:], src_ap, T.sem["rz%d" % t], T.sem.ls, a[1], a[0], m),
           sem=("ls", len(e)))
        frm = cores[(rank - (1 if t == 1 else 2)) % nr]
        op("n", 3500, ("sent%d" % t,), ("Z%d" % t,), sem=("rz%d" % t, len(engs(frm, core))))

    op("g", 180, (), ("pI",), lambda: g.iota(T.pc[:, 0:1], [[1, 1]], 0, 1))
    op("g", 380, (), ("cg",), lambda: g.iota(T.cg[:, 0:128], [[1, 8], [0, 16]], 0, 0))
    op("g", 380, (), ("cm",), lambda: g.iota(T.cm[:], [[0, 8], [1, 16]], 0, 0))
    op("g", 380, (), ("cI",), lambda: g.iota(T.cI[:], [[1, 128]], 0, 0))
    memset(T.ONES[:], 1.0, 128, ("ONES",))
    memset(T.HALF[:], 0.5, 128, ("HALF",))
    memset(T.rows[:, 0:128], -2080.0, 128, ("rowA",))
    memset(T.rows[:, 128:256], 2336.0, 128, ("rowB",))
    memset(T.c[:], 0.0, 128, ("c",))
    memset(T.h12[:], 0.0, 512, ("h12",))
    memset(T.h3[:], 0.0, 256, ("h3",))
    pc, pf = T.pc, T.pf
    pi = pc[:, 0:1]
    copy(pf[:, 0:1], pi, 1, ("pI",), ("f0",))
    ts(pc[:, 1:2], pi, 4, OP.logical_shift_right, 1, ("pI",), ("i1",))
    ts(pc[:, 2:3], pi, 15, OP.bitwise_and, 1, ("pI",), ("i2",))
    copy(pf[:, 1:2], pc[:, 1:2], 1, ("i1",), ("f1",))
    copy(pf[:, 2:3], pc[:, 2:3], 1, ("i2",), ("f2",))
    cI = T.cI[:]
    op("g", 1050, (), ("cg5",), lambda: g.iota(T.cg[:, 128:640], [[1, 32], [0, 16]], 0, 0))
    cg, cm = T.cg[:, 0:128], T.cm[:]
    ts(T.BO[:], cg, pf[:, 1:2], OP.is_equal, 128, ("cg", "f1"), ("BO",))
    ts(pc[:, 8:9], T.WI[:], 4032, OP.bitwise_and, 1, ("WI",), ("i8",))
    ts(pc[:, 9:10], T.WI[:], 63, OP.bitwise_and, 1, ("WI",), ("i9",))
    copy(pf[:, 8:9], pc[:, 8:9], 1, ("i8",), ("f8",))
    copy(pf[:, 9:10], pc[:, 9:10], 1, ("i9",), ("f9",))
    ts(T.WH[:], T.BO[:], pf[:, 8:9], OP.mult, 128, ("BO", "f8"), ("WH",))
    ts(T.WL[:], T.BO[:], pf[:, 9:10], OP.mult, 128, ("BO", "f9"), ("WL",))
    ts(pc[:, 10:11], T.WI[:], 37, OP.mult, 1, ("WI",), ("i10",))
    ts(pc[:, 11:12], pc[:, 10:11], 992, OP.bitwise_and, 1, ("i10",), ("i11",))
    ts(pc[:, 12:13], pc[:, 10:11], 31, OP.bitwise_and, 1, ("i10",), ("i12",))
    copy(pf[:, 11:12], pc[:, 11:12], 1, ("i11",), ("f11",))
    copy(pf[:, 12:13], pc[:, 12:13], 1, ("i12",), ("f12",))
    act(T.VH[:], T.BO[:], AF.Copy, 128, ("BO", "f11"), ("VH",), scale=pf[:, 11:12])
    act(T.VL[:], T.BO[:], AF.Copy, 128, ("BO", "f12"), ("VL",), scale=pf[:, 12:13])
    ts(T.MK[:, 0:128], cm, pf[:, 2:3], OP.is_equal, 128, ("cm", "f2"), ("MKa",))
    act(T.MK[:, 128:256], T.MK[:, 0:128], AF.Copy, 128, ("MKa",), ("MK",))
    ts(T.RS[:, 0:128], cm, 0.0, OP.is_gt, 128, ("cm",), ("RSa",))
    act(T.RS[:, 128:256], T.RS[:, 0:128], AF.Copy, 128, ("RSa",), ("RS",))
    ts(T.I[:], cI, pf[:, 0:1], OP.is_equal, 128, ("cI", "f0"), ("I",))
    ts(T.R8[:], T.cI[:, 0:8], pf[:, 1:2], OP.is_equal, 8, ("cI", "f1"), ("R8",))
    ts(T.tf[:], T.RS[:, 0:128], 0.5, OP.mult, 128, ("RSa",), ("tf",))
    ts(T.tf2[:], T.RS[:, 0:128], -512.0, OP.mult, 128, ("RSa",), ("tf2",), s2=512.0, o2=OP.add)
    scan(T.mb[:], T.tf[:], T.tf2[:], OP.mult, OP.add, 128, ("tf", "tf2"), ("mb",))
    tt(T.tf[:], T.mb[:], T.I[:], OP.mult, 128, ("mb", "I"), ("tf",))
    op("v", dv(128), ("tf",), ("f5",), lambda: V.tensor_reduce(pf[:, 5:6], T.tf[:], AxisListType.X, OP.add))
    ts(pf[:, 6:7], pf[:, 2:3], 8.0, OP.is_ge, 1, ("f2",), ("f6",))
    ts(pf[:, 7:8], pf[:, 6:7], 63.75, OP.mult, 1, ("f6",), ("f7",), s2=0.25, o2=OP.add)
    tt(pf[:, 10:11], pf[:, 7:8], pf[:, 5:6], OP.mult, 1, ("f7", "f5"), ("f10",))
    ts(pc[:, 13:14], pc[:, 1:2], 1, OP.bitwise_and, 1, ("i1",), ("i13",))
    ts(pf[:, 13:14], pf[:, 2:3], 10.0, OP.is_lt, 1, ("f2",), ("f13",))
    tt(pf[:, 14:15], pf[:, 13:14], pc[:, 13:14], OP.mult, 1, ("f13", "i13"), ("f14",))
    tt(pf[:, 15:16], pf[:, 13:14], pf[:, 14:15], OP.subtract, 1, ("f13", "f14"), ("f15",))
    ts(pf[:, 16:18], pf[:, 14:16], 1.0 / 256, OP.mult, 2, ("f14", "f15"), ("f16",))
    ts(pf[:, 18:20], pf[:, 14:16], -1.0, OP.mult, 2, ("f14", "f15"), ("f18",))
    ts(T.tf[:, 0:8], T.cI[:, 0:8], 16.0, OP.mult, 8, ("cI", "tf"), ("tf",), s2=1024.0, o2=OP.add)
    ts(pf[:, 48:56], T.tf[:, 0:8], pf[:, 2:3], OP.add, 8, ("tf", "f2"), ("iw",))
    ts(pc[:, 3:4], pi, 31, OP.bitwise_and, 1, ("pI",), ("i3",))
    copy(pf[:, 3:4], pc[:, 3:4], 1, ("i3",), ("f3",))
    ts(pf[:, 4:5], pf[:, 0:1], 32.0, OP.mult, 1, ("f0",), ("f4",))
    ts(T.SEL[:], T.cg[:, 128:640], pf[:, 3:4], OP.is_equal, 512, ("cg5", "f3"), ("SEL",), s2=-1.0, o2=OP.mult)
    act(T.G16[:], T.R8[:], AF.Copy, 8, ("R8",), ("G16",), scale=16.0)
    act(T.KC[:], T.BO[:], AF.Copy, 128, ("BO",), ("KC",), scale=128.0)
    ts(T.rows[:, 512:640], cm, -1.0, OP.mult, 128, ("cm",), ("rowR",), s2=15.0, o2=OP.add)
    ts(T.rows[:, 672:688], T.cI[:, 0:16], 8.0, OP.is_ge, 16, ("cI",), ("rowZ",), s2=-8.0, o2=OP.mult)
    tt(T.rows[:, 656:672], T.cI[:, 0:16], T.rows[:, 672:688], OP.add, 16, ("cI", "rowZ"), ("rowY",))
    ts(T.rows[:, 640:656], T.rows[:, 656:672], 256.0, OP.mult, 16, ("rowY",), ("rowX",))

    def cst(name, t):
        return T[name][:, 128 * t:128 * t + 128]

    def scaled(name, val, t=None):
        out = T[name][:] if t is None else cst(name, t)
        act(out, T.I[:], AF.Copy, 128, ("I",), (name if t is None else name + str(t),), scale=val)

    for name, val in (("KF", THR), ("I16", 16.0), ("nI16", -16.0), ("nI", -1.0), ("nI256", -256.0)):
        scaled(name, val)
    act(T.D32[:], T.I[:], AF.Copy, 128, ("I", "f4"), ("D32",), scale=pf[:, 4:5])
    for t in range(NST):
        scaled("HI", 4096.0 * (8 + t), t)
        if t:
            scaled("TI", float(t), t)
    for j in range(2):
        memset(T["X%d" % j][:, 0:4 * XS:XS], -64.0, 4, ["Xs%d" % j])
        memset(T["X%d" % j][:, 4 * XS::XS], -1.0, 4, ["Xt%d" % j])
    tw = T.tw
    ts(tw[:, 64:72], T.cI[:, 0:8], 0.0, OP.is_equal, 8, ("cI",), ("d1",))
    for nm_, base_, o in (("n", 1.0 / 64, 0), ("p", 64.0, 24)):
        memset(tw[:, 72 + o:80 + o], base_, 8, ("d0" + nm_,))
        scan(tw[:, 80 + o:88 + o], tw[:, 72 + o:80 + o], tw[:, 64:72], OP.mult, OP.add, 8, ("d0" + nm_, "d1"), ("pw" + nm_,))
        tt(tw[:, 88 + o:96 + o], tw[:, 80 + o:88 + o], T.R8[:], OP.mult, 8, ("pw" + nm_, "R8"), ("px" + nm_,))
    op("v", dv(8), ("pxn",), ("f57",), lambda: V.tensor_reduce(pf[:, 57:58], tw[:, 88:96], AxisListType.X, OP.add))
    op("v", dv(8), ("pxp",), ("f58",), lambda: V.tensor_reduce(pf[:, 58:59], tw[:, 112:120], AxisListType.X, OP.add))
    ts(tw[:, 8:24], T.cm[:, 0:16], pf[:, 2:3], OP.is_gt, 16, ("cm", "f2"), ("wt0",), s2=1.9375, o2=OP.mult)
    ts(T.rows[:, 900:916], tw[:, 8:24], 0.0625, OP.add, 16, ("wt0", "f57"), ("WT",), s2=pf[:, 57:58], o2=OP.mult)
    act(T.MK2[:], T.MK[:, 0:128], AF.Copy, 128, ("MKa", "f58"), ("MK2",), scale=pf[:, 58:59])
    ts(pf[:, 20:21], pf[:, 2:3], 1.0, OP.add, 1, ("f2",), ("f20",))
    ts(T.tf2[:], cm, 16.0, OP.mult, 128, ("cm", "f20"), ("tf2",), s2=pf[:, 20:21], o2=OP.add)
    tt(T.Kc[:], T.tf2[:], T.BO[:], OP.mult, 128, ("tf2", "BO"), ("Kc",))
    act(T.Kn[:], T.Kc[:], AF.Copy, 128, ("Kc",), ("Kn",), scale=-1.0)
    ts(pc[:, 4:5], pi, 3, OP.logical_shift_right, 1, ("pI",), ("i4",))
    ts(pc[:, 5:6], pi, 7, OP.bitwise_and, 1, ("pI",), ("i5",))
    copy(pf[:, 21:22], pc[:, 5:6], 1, ("i5",), ("f21",))
    for j in range(6):
        ts(pf[:, 22 + j:23 + j], pc[:, 4:5], float(j), OP.is_equal, 1, ("i4",), ("f%d" % (22 + j),))
    tt(pf[:, 32:35], pf[:, 22:25], pf[:, 25:28], OP.add, 3, ["f%d" % j for j in range(22, 28)], ("f32",))
    tt(pf[:, 35:37], pf[:, 32:34], pf[:, 33:35], OP.subtract, 2, ("f32",), ("f35",))
    tt(pf[:, 37:38], pf[:, 32:33], pf[:, 34:35], OP.subtract, 1, ("f32",), ("f37",))
    for j in range(3):
        ts(T.SM[:, 8 * j:8 * j + 8], T.cI[:, 0:8], pf[:, 21:22], OP.is_equal, 8, ("cI", "f21", "f35", "f37"), ("M1%d" % j,),
           s2=pf[:, 35 + j:36 + j], o2=OP.mult)
    memset(T.SM[:, 24:32], 0.0, 8, ("M13",))
    memset(T.SM[:, 32:120], 0.0, 88, ("RB",))
    copy(T.SM[:, 72:80], T.R8[:], 8, ("R8",), ("RB",), x=0.5)
    ts(pf[:, 38:44], pf[:, 22:28], 0.5, OP.mult, 6, ["f%d" % j for j in range(22, 28)], ("f38",))
    tt(pf[:, 46:47], pf[:, 25:26], pf[:, 26:27], OP.add, 1, ("f25", "f26"), ("f46",))
    ts(pf[:, 29:30], pf[:, 46:47], -2.0, OP.mult, 1, ("f46",), ("f29",))
    tt(pf[:, 44:45], pf[:, 39:40], pf[:, 38:39], OP.subtract, 1, ("f38",), ("f44",))
    tt(pf[:, 28:29], pf[:, 44:45], pf[:, 29:30], OP.add, 1, ("f44", "f29"), ("f28",))
    tt(pf[:, 45:46], pf[:, 39:40], pf[:, 40:41], OP.add, 1, ("f38",), ("f45",))
    tt(pf[:, 30:31], pf[:, 29:30], pf[:, 45:46], OP.subtract, 1, ("f29", "f45"), ("f30",))
    ts(T.CO1[:], cg, pf[:, 21:22], OP.is_equal, 128, ("cg", "f21", "f28"), ("CO1",), s2=pf[:, 28:29], o2=OP.mult)
    ts(T.CO2[:], cg, pf[:, 21:22], OP.is_equal, 128, ("cg", "f21", "f30"), ("CO2",), s2=pf[:, 30:31], o2=OP.mult)

    P0, P1, P2, P3, P4, P5, P6, P7 = [T["P%d" % i] for i in range(8)]
    one1 = T.ONES[0:1, :]

    def zap(t):
        return T.ZB[:, 0:128] if t == 0 else T["Z%d" % t][:]

    def zk(t):
        return "ZB" if t == 0 else "Z%d" % t

    def prep(t):
        z, k, d = zap(t), zk(t), t % 2
        for j in range(4):
            pcopy(T.zr4[:, j::4], z[:, 0:64], (k,), ("zr4%d" % j,), 64)
        for j in range(4):
            pcopy(T["zr%d" % d][:, j::4], T.zr4[:], ["zr4%d" % i for i in range(4)], ("zr%d" % d,) if j == 3 else ("zq%d%d" % (d, j),), 256)
        mm(256, (k, "WH", "WL"), "P6", (P6[:, 0:128], T.WH[:], z, True, False), (P6[:, 0:128], T.WL[:], z, False, True))
        mm(256, (k, "VH", "VL"), "P6", (P6[:, 128:256], T.VH[:], z, True, False), (P6[:, 128:256], T.VL[:], z, False, True))
        copy(T.Ui[:], P6[:, 0:128], 128, (), ("Ui",), banks=("P6",))
        ts(T.u[:], T.Ui[:], 4095, OP.bitwise_and, 128, ("Ui",), ("u",))
        tt(T.sq[:], T.u[:], T.u[:], OP.mult, 128, ("u",), ("sq",))
        ts(T.s5[:], T.sq[:], 5, OP.logical_shift_right, 128, ("sq",), ("s5",))
        tt(P6[:, 256:384], T.s5[:], P6[:, 128:256], OP.add, 128, ("s5",), ("base",), banks=("P6",), x=1.0)
        sw = T["sw%d" % d]
        tt(T.mb[:], P6[:, 256:384], T.MK[:, 0:128], OP.mult, 128, ("base", "MKa"), ("mb",), banks=("P6",), x=1.0)
        scan(sw[:], T.RS[:, 0:128], T.mb[:], OP.mult, OP.add, 128, ("RSa", "mb"), ("sw%d" % d,))
        mm(128, (k, "I"), "P6", (P6[:, 384:512], z, T.I[:], True, True))
        act(T["zT%d" % d][:], P6[:, 384:512], AF.Copy, 128, (), ("zT%d" % d,), banks=("P6",))

    def dups(t):
        z, k, d = zap(t), zk(t), t % 2
        ts(T.bb[:], P6[:, 256:384], pf[:, 5:6], OP.mult, 128, ("base", "f5"), ("bb",), banks=("P6",))
        if t <= NST - 3:
            ts(T.ub[:], P6[:, 0:128], pf[:, 10:11], OP.mult, 128, ("f10",), ("ub",), banks=("P6",))
            ts(T.ubm[:], T.ub[:], 128, OP.bitwise_and, 128, ("ub",), ("ubm",))
            bt = T["BT%d" % d]
            ts(bt[:, 0:128], T.ubm[:], -1.0 / 128, OP.mult, 128, ("ubm",), ("bta%d" % d,))
            pcopy(bt[:, 128:256], bt[:, 0:128], ("bta%d" % d,), ("BT%d" % d,))
        ts(T.bbm[:], T.bb[:], 512, OP.bitwise_and, 128, ("bb",), ("bbm",))
        ts(T.BD[:], T.bbm[:], pf[:, 16:17], OP.mult, 128, ("bbm", "f16", "f18"), ("BD",), s2=pf[:, 18:19], o2=OP.add)
        ts(T.BE[:], T.bbm[:], pf[:, 17:18], OP.mult, 128, ("bbm", "f16", "f18"), ("BE",), s2=pf[:, 19:20], o2=OP.add)
        for h in range(2):
            for j in range(2):
                calls = []
                for i in range(2):
                    bx = (T.BD if i else T.BE)[64 * h + 32 * j:64 * h + 32 * j + 32, :]
                    calls.append((P0[:, 256 * j + 128 * i:256 * j + 128 * i + 128], bx, bx, True, True))
                mm(256, ("BD", "BE"), "P0", *calls, grp=("gdup",), hard=bool(j))
            act(T.EQ[:, 512 * h:512 * h + 512], P0[:], AF.Relu, 512, (), ("EQ%d" % h,), bias=-9.0, banks=("P0",))
        mm(512, ("EQ0", "EQ1", "WT"), "P0",
           *[(P0[:, 16 * j:16 * j + 16], T.EQ[:, 128 * j:128 * j + 128], T.rows[:, 900:916], True, True) for j in range(8)])
        tt(T.DM[:], P0[:, 0:128], T.MK2[:], OP.mult, 128, ("MK2",), ("DM",), banks=("P0",), x=1.0)
        mm(64, ("DM", "R8"), "P0", (P0[:, 128:136], T.DM[:], T.R8[:], True, True))
        act(T.dmin[:], P0[:, 128:136], AF.Sign, 8, (), ("dmin",), bias=-1.75, banks=("P0",))
        tt(T["nwi%d" % d][:], T.dmin[:], pf[:, 48:56], OP.mult, 8, ("dmin", "iw"), ("nwi%d" % d,))

    def voff(t):
        d = t % 2
        if t == 0:
            copy(T.vi[:], T.sw0[:, 15::16], 8, ("sw0",), ("vi",))
        else:
            ts(T.vi[:], T["sw%d" % d][:, 15::16], pf[:, 63:64], OP.add, 8, ("sw%d" % d, "A"), ("vi",))
        ts(T.vm[:, 8 * d:8 * d + 8], T.vi[:], 1023, OP.bitwise_and, 8, ("vi",), ("vm%d" % d,))
        copy(T["goff%d" % d][:], T.vm[:, 8 * d:8 * d + 8], 8, ("vm%d" % d,), ("goff%d" % d,))

    def soff(t):
        d = t % 2
        tt(T.so[:], T.vm[:, 8 * d:8 * d + 8], T["nwi%d" % d][:], OP.max, 8, ("vm%d" % d, "nwi%d" % d), ("so",))
        copy(T["soff%d" % d][:], T.so[:], 8, ("so",), ("soff%d" % d,))

    def main(t):
        d = t % 2
        z, k = zap(t), zk(t)
        last = t == NST - 1
        go, gk = T["goff%d" % d][:, 0:8], "goff%d" % d
        X, xk = T["X%d" % d], "X%d" % d
        win = T.BK[:, 0:1024]
        qb = {"bias": 129.5 + 2.0 ** -14, "scale": 1.0 / 4096}
        if t == 0:
            copy(T.bi[:], T.BKI[:].indirect(go), 128, ("BKI", gk), ("bi",), x=1.6)
            copy(T.nb[:], T.bi[:], 128, ("bi",), ("nb",))
            act(T.qt[:], T.nb[:], AF.Identity, 128, ("nb",), ("qt",), **qb)
            copy(T.BK[:, 0:1024], T.BKI[:], 1024, ("BKI",), ("BK",))
        else:
            copy(T.bi[:], win.indirect(go), 128, ("BK", gk), ("bi",), x=1.6)
            act(T.qt[:], win.indirect(go), AF.Identity, 128, ("BK", gk), ("qt",), x=1.6, **qb)
        ts(T.bm[:], T.bi[:], 4095, OP.bitwise_and, 128, ("bi",), ("bm",))
        copy(T.b16[:], T.bm[:], 128, ("bm",), ("b16",))
        act(T.Fs[:], T.qt[:], AF.Sign, 128, ("qt",), ("Fs",), bias=-(131.5 + t))
        for c in range(8):
            off = T.b16[:, 16 * c:16 * c + 16]
            out = X[:, XS * c + 1:XS * c + 257]
            if c < 4:
                tt(out, T.G[:].indirect(off), T["zr%d" % d][:, 256 * c:256 * c + 256], OP.subtract, 256,
                   ("G", "b16", "zr%d" % d) + tuple("zq%d%d" % (d, j) for j in range(3)), (xk + str(c),), x=1.6)
            else:
                act(out, T.G[:].indirect(off), AF.Copy, 256, ("G", "b16"), (xk + str(c),), x=1.6)
        mm(256, ("qt", "I16", "ONES", "rowA"), "P7", (P7[:, 128:256], one1, T.rows[0:1, 0:128], True, False),
           (P7[:, 128:256], T.qt[:], T.I16[:], False, True))
        mm(384, ("qt", "nI16", "ONES", "rowB", "rowR"), "P7", (P7[:, 256:384], one1, T.rows[0:1, 128:256], True, False),
           (P7[:, 256:384], one1, T.rows[0:1, 512:640], False, False), (P7[:, 256:384], T.qt[:], T.nI16[:], False, True))
        if True:
            mm(64, ("Fs", "R8"), "P7", (P7[:, 384:392], T.Fs[:], T.R8[:], True, True))
        act(T.ivm[:], T.IM[:, 0:1024].indirect(go), AF.Identity, 128, ("IM", gk), ("ivm",), bias=-1.0, x=1.6)
        mm(256, (k, "ivm", "I", "nI"), "P7", (P7[:, 0:128], T.I[:], z, True, False), (P7[:, 0:128], T.nI[:], T.ivm[:], False, True))
        act(T.Sg[:], P7[:, 0:128], AF.Sign, 128, (), ("Sg",), bias=-1.5, banks=("P7",))
        mm(256, ("Fs", "KF", "rowR", "ONES"), "P5", (P5[:, 0:128], one1, T.rows[0:1, 512:640], True, False),
           (P5[:, 0:128], T.Fs[:], T.KF[:], False, False), grp=("gkey",))
        def dist(e):
            lo, hi = DIST[e]
            if hi > lo:
                mm(16 * max(hi - lo, 8), ["AB%d%d" % (i, j) for i in range(lo // 32, hi // 32) for j in range(2)] + ["G16"], "P5",
                   *[(P5[lo:hi, kk:128:16], T.AB[:, 16 * lo + kk:16 * hi:16], T.G16[:], False, kk == 15) for kk in range(16)],
                   grp=("gkey",))
        for e in range(4):
            if e < 2:
                for c in (2 * e, 2 * e + 1):
                    act(T.AB[:, 256 * c:256 * c + 256], X[:, XS * c + 1:XS * c + 257], AF.Abs, 256, (xk + str(c),), ("AB%d%d" % (e, c % 2),))
                dist(e)
                continue
            bank = "P%d" % (1 + e % 2)
            pb = T[bank]
            zt = T["zT%d" % d][32 * e:32 * e + 32, :]
            mm(512, ("zT%d" % d, "SEL"), bank, (pb[:], zt, T.SEL[32 * e:32 * e + 32, :], True, False), grp=("g" + bank,))
            for j in range(2):
                c = 2 * e + j
                mm(256, (xk + str(c), "I"), bank, (pb[:, 256 * j:256 * j + 256], T.I[:], X[:, XS * c + 1:XS * c + 257], False, j == 1), grp=("g" + bank,))
            act(T.AB[:, 512 * e:512 * e + 512], pb[:], AF.Abs, 512, (), ("AB%d0" % e, "AB%d1" % e), banks=(bank,))
            dist(e)
        dups(t)
        soff(t)
        pcopy(T.G[:, t::32], z, (k,), ("G",))
        mm(192, ("Sg", "KC", "R8"), "P7", (P7[:, 0:128], T.Sg[:], T.KC[:], True, True), (P7[:, 392:400], T.Sg[:], T.R8[:], True, True))
        act(T.cap[:], P7[:, 0:128], AF.Relu, 128, (), ("cap",), banks=("P7",))
        ts(T.sk[:], P7[:, 392:400], 1.0, OP.is_ge, 8, (), ("sk",), banks=("P7",))
        tt(P7[:, 128:256], P7[:, 128:256], T.cap[:], OP.min, 128, ("cap",), ("q16s",), banks=("P7",), x=1.0)
        ts(T.hm[:], P7[:, 384:392], -12.0, OP.min, 8, (), ("hm",), s2=16.0, o2=OP.add, banks=("P7",))
        tt(T.hv[:], T.hm[:], T.sk[:], OP.mult, 8, ("hm", "sk"), ("hv",))
        if last:
            load(T.ygeno[:], T.G[:], ("yg",), 7000, r=("G",))
        else:
            mm(64, ("hv", "HALF"), "P7", (P7[:, 400:408], T.HALF[:], T.hv[:], True, True))
            op("v", dv(8), (), ("A",), lambda: V.tensor_reduce(pf[:, 63:64], P7[:, 400:408], AxisListType.X, OP.add), banks=("P7",))
            prep(t + 1)
            voff(t + 1)
        key = P5[:, 0:128]
        RS = T.RS[:, 0:128]
        scan(T.ab[:, 0:128], RS, key, OP.mult, OP.max, 128, ("RSa",), ("a",), banks=("P5",))
        tt(T.c[:, 1:128], T.ab[:, 0:127], P5[:, 1:128], OP.min, 128, ("a",), ("c",), banks=("P5",), x=1.0)
        scan(T.ab[:, 128:256], T.c[:], RS, OP.max, OP.mult, 128, ("c", "RSa"), ("b",))
        ts(T.h12[:, 0::16], T.ab[:, 15::16], THR, OP.max, 16, ("a", "b"), ("h12",))
        scan(T.hb12[:], T.RS[:], T.h12[:], OP.mult, OP.add, 256, ("h12", "RS"), ("hb12",))
        tt(T.W[:], key, T.hb12[:, 128:256], OP.is_ge, 128, ("hb12",), ("W",), banks=("P5",), x=1.0)
        tt(T.E1[:], key, T.hb12[:, 0:128], OP.is_ge, 128, ("hb12",), ("E1",), banks=("P5",), x=1.0)
        tt(T.wq[:], P7[:, 128:256], T.W[:], OP.mult, 128, ("W", "q16s"), ("wq",), banks=("P7",), x=1.0)
        tt(T.e2[:], P7[:, 256:384], T.wq[:], OP.add, 128, ("wq",), ("e2",), banks=("P7",), x=1.0)
        scan(T.s3[:], RS, T.e2[:], OP.mult, OP.max, 128, ("e2", "RSa"), ("s3",))
        copy(T.h3[:, 0::16], T.s3[:, 15::16], 8, ("s3",), ("h3",))
        scan(P5[:, 384:512], RS, T.h3[:], OP.mult, OP.add, 128, ("h3", "RSa"), ("hb3",), banks=("P5",))
        tt(T.S[:], T.e2[:], P5[:, 384:512], OP.is_equal, 128, ("e2", "hb3"), ("S",), banks=("P5",), x=1.0)
        mm(128, ("wq", "nI256"), "P7", (P7[:, 0:128], T.wq[:], T.nI256[:], True, True))
        calls = [(P5[:, 256:384], T.S[:], T.D32[:], True, False)]
        if t:
            calls.append((P5[:, 256:384], T.S[:], cst("TI", t), False, False))
        calls.append((P5[:, 256:384], T.S[:], cst("HI", t), False, True))
        tt(T.t1[:], T.bi[:], P7[:, 0:128], OP.add, 128, ("bi",), ("t1",), banks=("P7",), x=1.0)
        mm(384, ("S", "D32", "HI%d" % t) + (("TI%d" % t,) if t else ()), "P5", *calls)
        tt(T.nb[:], T.t1[:], P5[:, 256:384], OP.max, 128, ("t1",), ("nb",), banks=("P5",), x=1.0)
        so, sk_ = T["soff%d" % d][:, 0:8], "soff%d" % d
        copy(T.BK[:, 0:1152].indirect(so), T.nb[:], 128, ("nb", sk_), ("BK",), x=3.5)
        if last:
            load(T.ybank[:], T.BK[:, 0:1024], ("yb",), 4000, r=("BK",))
        mm(256, ("W", "E1", "I"), "P3", (P3[:, 0:128], T.E1[:], T.I[:], True, True), (P3[:, 128:256], T.W[:], T.I[:], True, True))
        act(T.WE[:], P3[:, 0:256], AF.Copy, 256, (), ("WE",), banks=("P3",))
        mm(384, ("WE", "Kc", "Kn"), "P3", (P3[:, 256:384], T.WE[:, 0:128], T.Kc[:], True, True),
           (P3[:, 384:512], T.WE[:, 128:256], T.Kc[:], True, False), (P3[:, 384:512], T.WE[:, 0:128], T.Kn[:], False, True))
        tt(T.L[:], P3[:, 256:512], T.MK[:], OP.mult, 256, ("MK",), ("L",), banks=("P3",), x=1.0)
        mm(256, ("L", "R8", "ONES", "rowX", "rowY"), "P3", (P3[:, 0:16], one1, T.rows[0:1, 640:656], True, False),
           (P3[:, 0:16], one1, T.rows[0:1, 656:672], False, False),
           (P3[:, 0:8], T.L[:, 0:128], T.R8[:], False, False), (P3[:, 8:16], T.L[:, 128:256], T.R8[:], False, True))
        copy(T.oXA[:], P3[:, 0:16], 16, (), ("oXA",), banks=("P3",))
        act(T.A12[:], X[:].indirect(T.oXA[:, 0:16]), AF.Copy, 256, ["oXA", "Xs%d" % d, "Xt%d" % d] + [xk + str(c) for c in range(8)], ("A12",), x=1.6)
        mm(384, ("A12", k, "I", "nI"), "P4", (P4[:, 0:256], T.I[:], T.A12[:], True, False),
           (P4[:, 64:128], T.nI[:], z[:, 64:128], False, False), (P4[:, 192:256], T.nI[:], z[:, 64:128], False, True))
        mm(256, ("A12", "I", "nI"), "P4", (P4[:, 256:384], T.I[:], T.A12[:, 128:256], True, False),
           (P4[:, 256:384], T.nI[:], T.A12[:, 0:128], False, True))
        act(T.Ps[:], P4[:, 0:384], AF.Sign, 384, (), ("Ps",), bias=-0.5, banks=("P4",))
        act(T.Ns[:], P4[:, 0:384], AF.Sign, 384, (), ("Ns",), bias=-0.5, scale=-1.0, banks=("P4",))

        def cnt(j, buf, i, first=False, last_=False):
            return (P4[0:48, 384:512], T.SM[:, 72 - 8 * j:120 - 8 * j], buf[:, 128 * i:128 * i + 128], first, last_)
        mm(384, ("Ps", "RB"), "P4", cnt(0, T.Ps, 0, True), cnt(3, T.Ps, 1), cnt(4, T.Ps, 2), grp=("gcnt",))
        mm(384, ("Ns", "RB"), "P4", cnt(1, T.Ns, 0), cnt(2, T.Ns, 1), cnt(5, T.Ns, 2, False, True), grp=("gcnt",))
        act(T.B[0:48, :], P4[0:48, 384:512], AF.Sign, 128, (), ("B",), bias=-1.0, banks=("P4",))
        mm(192, ("B", "M10", "M11", "M12", "M13", "hv", "I"), "P3", (P3[0:32, 0:128], T.SM[0:48, 0:32], T.B[0:48, :], True, True),
           (P3[32:40, 0:128], T.hv[:], T.I[:], True, True))
        act(T.XT[0:40, :], P3[0:40, 0:128], AF.Sign, 128, (), ("XT",), bias=-1.0, banks=("P3",))
        mm(256, ("XT", "CO1", "CO2"), "P0", (P0[:, 0:128], T.CO1[0:40, :], T.XT[0:40, :], True, True),
           (P0[:, 128:256], T.CO2[0:40, :], T.XT[0:40, :], True, True))
        bt = "BT%d" % d
        if t <= NST - 3:
            tt(T.C[:], P0[:, 0:256], T[bt][:], OP.is_equal, 256, (bt,), ("C",), banks=("P0",), x=1.0)
            tt(T.CD[:], T.C[:], P4[:, 0:256], OP.mult, 256, ("C",), ("CD",), banks=("P4",), x=1.0)
        act(T.F[:], P0[:, 0:256], AF.Relu, 256, (), ("F",), scale=-1.0, banks=("P0",))
        tt(T.FD[:], T.F[:], P4[:, 0:256], OP.mult, 256, ("F",), ("FD",), banks=("P4",), x=1.0)
        mm(384, ("FD", k, "I"), "P0", (P0[:, 256:384], T.I[:], z, True, False), (P0[:, 256:384], T.I[:], T.FD[:, 0:128], False, False),
           (P0[:, 256:384], T.I[:], T.FD[:, 128:256], False, True))
        tt(T.nim[:], T.ivm[:], P0[:, 256:384], OP.max, 128, ("ivm",), ("nim",), banks=("P0",), x=1.0)
        copy(T.IM[:, 0:1152].indirect(so), T.nim[:], 128, ("nim", sk_), ("IM",), x=3.5)
        if last:
            load(T.yimm[:], T.IM[:, 0:1024], ("yi",), 3500, r=("IM",))
        if t <= NST - 3:
            mm(384, ("CD", k, "I"), "P3", (P3[:, 256:384], T.I[:], z, True, False), (P3[:, 256:384], T.I[:], T.CD[:, 0:128], False, False),
               (P3[:, 256:384], T.I[:], T.CD[:, 128:256], False, True))
            cr = "CR%d" % t
            act(cst("CR", t), P3[:, 256:384], AF.Copy, 128, (), (cr,), banks=("P3",))
            send(cst("CR", t), cr, cores[(rank + 2) % nr], t + 2)

    send(T.ZB[:, 128:256], "ZB", cores[(rank + 1) % nr], 1)
    prep(0)
    voff(0)
    for t in range(NST):
        main(t)
    return ops


def depend(ops):
    lw, rd, bank, rdy, prev = {}, {}, {}, [], []
    lastq = {}
    for i, o in enumerate(ops):
        need, order = set(), set()
        for k in o["r"]:
            if k in lw:
                need |= lw[k]
            rd.setdefault(k, []).append(i)
        for k in o["w"]:
            if k in lw:
                need |= lw[k]
            need |= set(rd.get(k, ()))
        for k in o["w"]:
            lw[k] = {i}
            rd[k] = []
        for k in o["b"]:
            h = bank.setdefault(k, [None, set(), set()])
            if h[0] != o["q"]:
                h[0], h[1], h[2] = o["q"], h[2], set()
            need |= h[1]
            h[2].add(i)
        if o["q"] == "s":
            if o["q"] in lastq:
                order.add(lastq[o["q"]])
            lastq[o["q"]] = i
        need.discard(i)
        order.discard(i)
        rdy.append(need)
        prev.append(order)
    return rdy, prev


def schedule(q, dur, nxt, cnt, key):
    n = len(q)
    left = cnt[:]
    avail, start, fin, seq = [0.0] * n, [0.0] * n, [0.0] * n, []
    ready = {k: [] for k in "vatgsn"}
    free = dict.fromkeys("vatgsn", 0.0)
    for i in range(n):
        if left[i] == 0:
            ready[q[i]].append(i)
    best, dirty = {}, list("vatgsn")
    while len(seq) < n:
        for k in dirty:
            r = ready[k]
            if not r:
                best.pop(k, None)
                continue
            f = free[k]
            t0 = max(f, min([avail[i] for i in r]))
            bi, bp = -1, -1e18
            for i in r:
                if avail[i] <= t0 and key[i] > bp:
                    bp, bi = key[i], i
            best[k] = (t0, bi)
        k = min(best, key=lambda x: best[x])
        st, i = best[k]
        ready[k].remove(i)
        seq.append(i)
        start[i], fin[i] = st, st + dur[i]
        free[k] = st + 60 if k == "s" else (0.0 if k == "n" else fin[i])
        dirty = [k]
        for j, lag in nxt[i]:
            av = fin[i] + lag
            if av > avail[j]:
                avail[j] = av
            left[j] -= 1
            if left[j] == 0:
                ready[q[j]].append(j)
                if q[j] not in dirty:
                    dirty.append(q[j])
    return max(fin), seq, start, fin


TRIES = 1500


def improve(ops, need, order):
    rnd = np.random.RandomState(3)
    n = len(ops)
    q, dur = [o["q"] for o in ops], [o["dur"] for o in ops]
    nxt, prv = [[] for _ in range(n)], [[] for _ in range(n)]
    for i in range(n):
        for j in sorted(need[i] | order[i]):
            lag = (40 if q[i] == q[j] else 80) if j in need[i] else 60 - dur[j]
            nxt[j].append((i, lag))
            prv[i].append((j, lag))
    cur = [0.0] * n
    for i in range(n - 1, -1, -1):
        cur[i] = dur[i] + max([cur[j] + 40 for j, _ in nxt[i]], default=0.0)
    best = None
    for _ in range(TRIES):
        r = schedule(q, dur, nxt, [len(x) for x in prv], cur)
        for _ in range(4):
            key = schedule(q, dur, prv, [len(x) for x in nxt], r[3])[3]
            r2 = schedule(q, dur, nxt, [len(x) for x in prv], key)
            if best is None or min(r, r2)[0] < best[0]:
                best = r2 if r2[0] < r[0] else r
            if r2[0] >= r[0] - 1:
                break
            r = r2
        key = schedule(q, dur, prv, [len(x) for x in nxt], best[3])[3]
        sg = (100.0, 400.0, 1500.0)[int(rnd.randint(3))]
        cur = [key[i] + sg * float(x) for i, x in enumerate(rnd.normal(size=n))]
    return best


PLAN = {}


def rank_program(g, core, T, topo):
    rank = T.rank_of(core)
    if rank is None:
        return
    ops = build(g, T, topo, core)
    if "seq" not in PLAN:
        need, order = depend(ops)
        PLAN["need"] = need
        PLAN["end"], PLAN["seq"], PLAN["start"], PLAN["fin"] = improve(ops, need, order)
    need, seq = PLAN["need"], PLAN["seq"]
    queue = {"v": g.vector, "a": g.scalar, "t": g.tensor, "g": g, "s": g.sync}
    count, done, known, clock = {}, {}, {}, {}
    for i in seq:
        o = ops[i]
        q = o["q"]
        kn = known.setdefault(q, {}) if q != "n" else {}
        for j in sorted(need[i], key=lambda x: -x):
            s, v = done[j]
            if q == "t" and ops[j]["q"] == "t" and not o["hard"]:
                continue
            if kn.get(s, 0) >= v:
                continue
            if q != "n":
                queue[q].wait_ge(T.sem[s], v)
            for s2, v2 in clock[j].items():
                kn[s2] = max(kn.get(s2, 0), v2)
            kn[s] = max(kn.get(s, 0), v)
        ins = None
        for f in o["f"]:
            ins = f()
        if o["sem"] is None:
            s = CNT[q]
            count[s] = count.get(s, 0) + 1
            ins.then_inc(T.sem[s], 1)
        else:
            s, v = o["sem"]
            count[s] = count.get(s, 0) + v
            if q == "s":
                ins.then_inc(T.sem[s], v)
        done[i] = (s, count[s])
        clock[i] = {} if q == "n" else dict(kn)
    kn = known["g"]
    for s in count:
        if kn.get(s, 0) < count[s]:
            g.wait_ge(T.sem[s], count[s])
